import numpy as np, ml_dtypes
CORES = [2,3,42,43,82,83,122,123]
N = 8
BF = ml_dtypes.bfloat16
V, CAP, LB, RO = 2048, 128, 2, 3
L = N * V
PL = (np.arange(N)[:, None] * V + np.arange(V)).reshape(N, 1, 1, V)
def draw(rng, size):
    s = (N, 8, 16, V)
    t = PL + 1 + (size * rng.random(s) * rng.random(s)).astype(np.int64)
    t = np.where(t > L, np.minimum(PL + 1 + ((L - PL) * rng.random(s)).astype(np.int64), L), t); z = rng.random(s)
    return np.where(z < 0.12, 0, np.where(z < 0.121, L, t))
def sizes(rng):
    a = np.array([V >> 6, V >> 5, V >> 4, V >> 3, V >> 3, V >> 2, V >> 1, 2 * V])[rng.permutation(8)]
    return (a[:, None] * np.exp2(2 * rng.random((8, 16)) - 1)).reshape(1, 8, 16, 1)
def perms(rng):
    return np.argsort(rng.random((N, 8, 16, LB)), axis=2)
def pack(t, rt):
    return {"ends": np.ascontiguousarray(t.reshape(N, 128, V)).astype(np.int32), "rights": np.ascontiguousarray(rt.reshape(N, 128, LB)).astype(np.int32)}
def setup_inputs(rng):
    return pack(draw(rng, sizes(rng)), perms(rng))
def setup_inputs_room(rng):
    t = draw(rng, np.full((1, 8, 16, 1), V >> 4)); p = np.arange(V)
    for r in range(N):
        for g in range(8):
            for b in range(LB):
                v = np.where((p == V - 1) | (rng.random(V) < 0.3), 0, r * V + p + 1 + ((V - 1 - p) * rng.random(V)).astype(np.int64))
                o = rng.permutation(V); k = 0
                for q in range(r + 1, N):
                    n = int(rng.choice(np.array([0, 1, CAP - 1, CAP, CAP + 1, 2 * CAP])))
                    if r == 0 and q == 1 and b == 0: n = (CAP, CAP + 1, 2 * CAP, CAP - 1, 1, 0, CAP, CAP + 1)[g]
                    x = rng.integers(0, V, n)
                    if n > 1: x[0] = 0; x[n - 1] = V - 1
                    v[o[k:k + n]] = q * V + x; k += n
                t[r, g, b] = v
    return pack(t, perms(rng))
def setup_inputs_alike(rng):
    t = draw(rng, sizes(rng)); p = PL.reshape(-1)
    for g in (0, 2, 4, 6):
        s = np.array([V, 1, 16, V // 4] * 4)
        if g: s = s[rng.permutation(16)]
        t[:, g] = np.minimum((PL[:, 0] // s[None, :, None] + 1) * s[None, :, None], L)
    for g in (1, 3):
        for a in range(16):
            cut = np.append(np.sort(rng.integers(1, L, 40)), L)
            t[:, g, a] = cut[np.searchsorted(cut, p, side="right")].reshape(N, V)
    rt = rng.integers(0, 16, (N, 8, 16, LB)); rt[:, 0] = np.arange(LB); rt[:, 2] = rng.choice(np.array([0, 15]), (N, 16, LB))
    return pack(t, rt)
def setup_inputs_fails(rng):
    t = draw(rng, sizes(rng)); rt = perms(rng); q = 1 + rng.permutation(7); h = V // 2; e = (N - 1) * V
    t[rng.integers(0, N), :, :LB] = 0
    t[:, 0, :LB] = 0; t[:, q[0], :LB] = 0; t[:, q[1], :LB] = L
    t[:, q[2]] = np.where(rng.random((N, 1, V)) < 0.6, 0, t[:, q[2]]); t[:, q[3], LB:] = 0
    b = int(rng.integers(0, LB))
    t[:, q[4], b] = np.where(rng.random((N, V)) < 0.1, L, 0); rt[:, q[4], b] = rng.integers(LB, 16, (N, LB))
    for s in (q[5], q[6]):
        t[:N - 1, s, :LB] = 0; t[N - 1, s, :, :h] = 0; t[N - 1, s, 0, :h] = e + h + rng.integers(0, h, h)
        for r in range(N - 1):
            o = rng.permutation(V)[:CAP]; t[r, s, 0, o] = e + rng.integers(0, h, CAP)
        rt[:N - 1, s, :, 0] = rng.integers(1, 15, (N - 1, 16))
    t[N - 1, q[6], 15, :h] = L; rt[:N - 1, q[6], 0, 0] = 15
    return pack(t, rt)
def setup_inputs_far(rng):
    t = draw(rng, np.full((1, 8, 16, 1), 8 * L))
    t[:, :, :LB] = np.where(rng.random((N, 8, LB, V)) < 0.85, 0, t[:, :, :LB])
    for r in range(N - 1):
        o = rng.permutation(8)
        for q in range(r + 1, N):
            b = int(rng.integers(1, LB)); v = np.where(rng.random(V) < 0.04, L, q * V + rng.integers(0, V, V))
            t[r, o[q], b] = v; t[r, o[q], 0] = np.where(rng.random(V) < 0.04, v, t[r, o[q], 0])
    t[:, :, :LB, 0] = L - 1; t[:, :, :LB, V - 1] = ((np.arange(N) + 1) * V)[:, None, None]
    return pack(t, perms(rng))
def setup_inputs_spread(rng):
    u = rng.random((N, 8, 16, V)) * np.sqrt(rng.random((N, 8, 1, V)))
    t = np.minimum(PL + np.maximum(np.exp2(np.log2(L - PL) * u).astype(np.int64), 1), L)
    t = np.where(rng.random(t.shape) < rng.random((N, 8, 1, 1)) * 0.3, 0, t)
    return pack(t, rng.integers(0, 16, (N, 8, 16, LB)))
def check_inputs(d):
    bad = []; a = np.asarray(d["ends"]).astype(np.int64); b = np.asarray(d["rights"])
    if not np.all((a == 0) | ((a > PL.reshape(N, 1, V)) & (a <= L))): bad.append("range of ends")
    if np.min(b) < 0 or np.max(b) > 15: bad.append("range of rights")
    return bad
def reference(ends, rights):
    m = np.ascontiguousarray(ends.astype(np.int64).reshape(N, 8, 16, V).transpose(1, 2, 0, 3)).reshape(8, 16, L)
    rt = rights.astype(np.int64).reshape(N, 8, 16, LB).transpose(1, 2, 0, 3)
    own = (np.arange(L) // V)[None, :]
    for rnd in range(RO):
        new = m
        for b in range(LB):
            t = m[:, b]; good = (t > 0) & (t < L); to = np.where(good, t // V, N)
            for q in range(1, N):
                far = (to == q) & (own < q)
                h = far.reshape(8, N, V).astype(np.int64); before = np.add.accumulate(h, axis=2) - h
                good = good & ~(far & (before.reshape(8, L) >= CAP))
            c = np.take_along_axis(m, np.where(good, t, 0)[:, None, :], 2)
            c = np.where(good[:, None, :], c, 0)
            c = np.take_along_axis(c.reshape(8, 16, N, V), rt[:, :, :, b:b + 1], 1).reshape(8, 16, L)
            new = np.maximum(new, c)
        m = new
    return {"y": np.ascontiguousarray(m.reshape(8, 16, N, V).transpose(2, 0, 1, 3)).reshape(N, 128, V).astype(np.float32)}

@@ -1,0 +1,394 @@
+import numpy as np
+from concourse.bass import DstId, RemoteDMATransfer
+from concourse.mybir import AluOpType, ActivationFunctionType
+
+V, N, RO, CAP = 2048, 8, 3, 128
+SEG = CAP + 1
+Z = 8
+BLK = Z + 2 * V
+BW = Z + 2 * CAP
+WCOLS = BLK + 9 * BW
+LCOLS = V + 7 * CAP
+CHUNKS, PIECES = 4, 8
+ROUND_C = 1.5 * 2.0 ** 34
+
+SCRATCH = {
+    "ei": ("sbuf", [128, V], "int32"), "E0": ("sbuf", [128, V], "float32"), "E1": ("sbuf", [128, V], "float32"),
+    "xw": ("sbuf", [128, 256], "int32"), "win": ("sbuf", [128, WCOLS], "float32"),
+    "wl0": ("sbuf", [128, LCOLS], "float32"), "wl1": ("sbuf", [128, LCOLS], "float32"),
+    "ri": ("sbuf", [128, 2], "int32"), "rf": ("sbuf", [128, 2], "float32"), "rcol": ("sbuf", [128, 2], "float32"),
+    "iom": ("sbuf", [128, 128], "float32"), "iop": ("sbuf", [128, 1], "float32"), "iosx": ("sbuf", [128, 16], "float32"),
+    "ip32": ("sbuf", [128, 1], "int32"), "im32": ("sbuf", [128, 128], "int32"),
+    "p16i": ("sbuf", [128, 1], "int32"), "p15i": ("sbuf", [128, 1], "int32"),
+    "p16f": ("sbuf", [128, 1], "float32"), "p15f": ("sbuf", [128, 1], "float32"),
+    "mm": ("sbuf", [128, 128], "int32"), "mg": ("sbuf", [128, 128], "float32"), "tg": ("sbuf", [128, 128], "float32"),
+    "idf": ("sbuf", [128, 128], "float32"), "id128": ("sbuf", [128, 128], "float32"), "selx": ("sbuf", [128, 16], "float32"),
+    "idb": ("sbuf", [128, 128], "bfloat16"), "wa": ("sbuf", [128, 128], "bfloat16"), "wb": ("sbuf", [128, 128], "bfloat16"),
+    "xi": ("sbuf", [128, 128], "float32"), "d0": ("sbuf", [128, 7 * SEG], "bfloat16"),
+    "oh0": ("sbuf", [128, 7 * SEG], "bfloat16"), "oh1": ("sbuf", [128, 7 * SEG], "bfloat16"),
+    "sc0": ("sbuf", [128, 7 * SEG], "bfloat16"), "sc1": ("sbuf", [128, 7 * SEG], "bfloat16"),
+    "rl0": ("sbuf", [128, 7 * CAP], "bfloat16"), "rl1": ("sbuf", [128, 7 * CAP], "bfloat16"),
+    "roh": ("sbuf", [128, 256], "float32"), "sr": ("sbuf", [128, 256], "float32"), "srb": ("sbuf", [128, 256], "bfloat16"),
+    "srl": ("sbuf", [128, 7 * 256], "bfloat16"), "srf": ("sbuf", [128, 7 * 256], "float32"),
+    "xs": ("sbuf", [128, 256], "float32"), "qb": ("sbuf", [128, 256], "bfloat16"), "rqv": ("sbuf", [128, 256], "float32"),
+    "yv": ("sbuf", [128, 256], "float32"), "zv": ("sbuf", [128, 256], "float32"), "o16": ("sbuf", [128, 256], "uint16"),
+    "u1": ("sbuf", [128, 256], "float32"), "a1": ("sbuf", [128, 256], "float32"),
+    "si": ("sbuf", [128, 256], "int32"), "av": ("sbuf", [128, 256], "float32"), "a16": ("sbuf", [128, 256], "uint16"),
+    "lq": ("sbuf", [128, 7 * 16], "float32"), "lo": ("sbuf", [128, 7 * 16], "uint16"), "rpf": ("sbuf", [128, 7 * 256], "float32"),
+    "rp": ("sbuf", [128, 7 * 256], "uint16"), "ld": ("sbuf", [128, 7 * 256], "uint16"),
+    "rqb": ("dram", [7, 128, 16], "float32"), "rland": ("dram", [7, 128, 16], "float32"),
+}
+for _k in range(8):
+    SCRATCH["ps%d" % _k] = ("psum", [128, 512], "float32")
+SEMAPHORES = (["qV", "qT", "qS", "qG", "lri", "lx0", "lx1", "dq0", "dq1", "lsq", "lss", "sra"]
+              + ["le%d" % k for k in range(CHUNKS)] + ["st%d" % k for k in range(PIECES)]
+              + ["rq%d" % k for k in range(7)] + ["rp%d" % k for k in range(8)] + ["ls%d" % k for k in range(7)] + ["lw%d" % k for k in range(7)])
+
+ADD, SUB, MUL, MAX, MIN, EQ, GT = (AluOpType.add, AluOpType.subtract, AluOpType.mult, AluOpType.max, AluOpType.min,
+                                   AluOpType.is_equal, AluOpType.is_gt)
+ACT = ActivationFunctionType
+
+
+def out_engines(topo, cores, q):
+    far = [c for c in cores if topo.chip(c) != topo.chip(cores[q])]
+    return topo.engines(cores[q], far[0])
+
+
+def width(topo, cores, p):
+    n, w = len(out_engines(topo, cores, p)), 1
+    while 2 * w * max(N - 1 - p, 1) <= n:
+        w *= 2
+    return w
+
+
+def rank_program(g, core, T, topo):
+    r = T.rank_of(core)
+    if r is None:
+        return
+    cores = T.cores
+    later = list(range(r + 1, N))
+    nq, nr = len(later), r
+    Q = {"V": g.vector, "T": g.tensor, "S": g.scalar, "Y": g.sync, "G": g}
+    total, clock, snap, acc, bank = {}, {q: {} for q in Q}, {}, {}, {}
+
+    def need(q, sem, val):
+        ck = clock[q]
+        if ck.get(sem, 0) >= val:
+            return
+        Q[q].wait_ge(T.sem[sem], val)
+        ck[sem] = val
+        for k, v in snap.get((sem, val), {}).items():
+            if ck.get(k, 0) < v:
+                ck[k] = v
+
+    def order(q, reads, writes, banks, extra):
+        want = {}
+
+        def add(tok):
+            if want.get(tok[0], 0) < tok[1]:
+                want[tok[0]] = tok[1]
+        for (b, lo, hi) in reads:
+            for e in acc.get(b, []):
+                if e[4] and e[0] < hi and lo < e[1]:
+                    add(e[2])
+        for (b, lo, hi) in writes:
+            for e in acc.get(b, []):
+                if e[0] < hi and lo < e[1]:
+                    add(e[2])
+        for k in banks:
+            for oq, tok in bank.get(k, {}).items():
+                if oq != q:
+                    add(tok)
+        for tok in extra:
+            add(tok)
+        for sem in sorted(want, key=lambda s: (s[0] != "q", s)):
+            need(q, sem, want[sem])
+
+    def note(q, tok, reads, writes, banks):
+        s = dict(clock[q])
+        s[tok[0]] = tok[1]
+        snap[tok] = s
+        for (b, lo, hi) in writes:
+            keep = [e for e in acc.get(b, []) if not (lo <= e[0] and e[1] <= hi)]
+            keep.append((lo, hi, tok, q, True))
+            acc[b] = keep
+        for (b, lo, hi) in reads:
+            keep = [e for e in acc.get(b, []) if e[4] or e[3] != q or (e[0], e[1]) != (lo, hi) or e[2][0] != tok[0]]
+            keep.append((lo, hi, tok, q, False))
+            acc[b] = keep
+        for k in banks:
+            bank.setdefault(k, {})[q] = tok
+
+    def op(q, fn, reads=(), writes=(), banks=(), extra=()):
+        order(q, reads, writes, banks, extra)
+        sem = "q" + q
+        total[sem] = total.get(sem, 0) + 1
+        fn(Q[q]).then_inc(T.sem[sem], 1)
+        note(q, (sem, total[sem]), reads, writes, banks)
+        return (sem, total[sem])
+
+    def dmas(q, sem, items, extra=()):
+        tok = (sem, total.get(sem, 0) + 16 * len(items))
+        total[sem] = tok[1]
+        for (o, i, rd, wr) in items:
+            order(q, rd, wr, (), extra)
+            Q[q].dma_start(o, i).then_inc(T.sem[sem], 16)
+        for (o, i, rd, wr) in items:
+            note(q, tok, rd, wr, ())
+        return tok
+
+    def tokens(sem, n):
+        total[sem] = total.get(sem, 0) + n
+        return (sem, total[sem])
+
+    def ps(k, lo, hi):
+        return T["ps%d" % k][:, lo:hi]
+
+    def rem_mask(engs):
+        m = 0
+        for e in engs:
+            m |= 1 << e
+        return m
+
+    def R(name, lo=0, hi=1 << 20):
+        return (name, lo, min(hi, SCRATCH[name][1][-1]))
+
+    pool = out_engines(topo, cores, r)
+
+    def to_later(src, dst, remote, local):
+        w, transfers = width(topo, cores, r), []
+        for k, q in enumerate(later):
+            rid, pid, _s = topo.addr(cores[q])
+            transfers.append(RemoteDMATransfer(dst_ids=[DstId(rid=rid, pnc=pid)], dma_engine_mask=rem_mask(pool[k * w:(k + 1) * w]),
+                                               remote_sem=T.sem[remote], src=src(k), dst=dst, alu_op=0))
+        g.remote_dma_fused(transfers, local_sem=T.sem[local])
+        tokens(local, w * nq)
+
+    CW = V // CHUNKS
+    dmas("S", "lri", [(T.ri[:], T.rights[:], (), [R("ri")])])
+    for b in range(2):
+        dmas("Y" if b == 0 else "S", "lx%d" % b,
+             [(T.xw[:, 128 * b + 16 * s:128 * b + 16 * s + 16], T.ends[16 * s + b:16 * s + b + 1, :], (),
+               [R("xw", 128 * b + 16 * s, 128 * b + 16 * s + 16)]) for s in range(8)])
+    for k in range(CHUNKS):
+        lo, hi = k * CW, (k + 1) * CW
+        dmas("Y" if k % 2 == 0 else "S", "le%d" % k, [(T.ei[:, lo:hi], T.ends[:, lo:hi], (), [R("ei", lo, hi)])])
+
+    def iota(name, pat, base, cm, lo, hi, f32=True):
+        if f32:
+            op("G", lambda e: e.iota(T[name][:, lo:hi], pat, base, cm, allow_small_or_imprecise_dtypes=True), (), [(name, lo, hi)])
+        else:
+            op("G", lambda e: e.iota(T[name][:, lo:hi], pat, base, cm), (), [(name, lo, hi)])
+
+    def ts(out, i, s1, s2, op0, op1, reads, writes, banks=(), q="V"):
+        if op1 is None:
+            return op(q, lambda e: e.tensor_scalar(out, i, s1, None, op0), reads, writes, banks)
+        return op(q, lambda e: e.tensor_scalar(out, i, s1, s2, op0, op1), reads, writes, banks)
+
+    def tt(out, i0, i1, o, reads, writes, banks=()):
+        return op("V", lambda e: e.tensor_tensor(out, i0, i1, o), reads, writes, banks)
+
+    def cp(out, i, reads, writes, banks=(), extra=()):
+        return op("V", lambda e: e.tensor_copy(out, i), reads, writes, banks, extra)
+
+    def act(out, i, f, reads, writes, banks=()):
+        return op("S", lambda e: e.activation(out, i, f), reads, writes, banks)
+
+    def mset(ap, val, wr):
+        op("V", lambda e: e.memset(ap, val), (), [wr])
+
+    iota("iop", [[1, 1]], 0, 1, 0, 1)
+    iota("ip32", [[1, 1]], 0, 1, 0, 1, False)
+    iota("iom", [[1, 128]], 0, 0, 0, 128)
+    if nq:
+        mset(T.d0[:], 1.0, R("d0"))
+        mset(T.oh0[:, 0:7 * SEG:SEG], 0.0, R("oh0"))
+        mset(T.oh1[:, 0:7 * SEG:SEG], 0.0, R("oh1"))
+        mset(T.d0[:, 0:7 * SEG:SEG], 0.0, R("d0"))
+        iota("im32", [[1, 128]], 0, 0, 0, 128, False)
+        iota("xi", [[16, 128]], 0, 0, 0, 128)
+    iota("iosx", [[1, 2], [16, 8]], 0, 0, 0, 16)
+    if nq:
+        for b in range(2):
+            iota("wl%d" % b, [[V, nq], [0, CAP]], V * (r + 1), 0, V, V + CAP * nq)
+    ts(T.p16i[:], T.ip32[:], 112, None, AluOpType.bitwise_and, None, [R("ip32")], [R("p16i")])
+    ts(T.p15i[:], T.ip32[:], 15, None, AluOpType.bitwise_and, None, [R("ip32")], [R("p15i")])
+    cp(T.p16f[:], T.p16i[:], [R("p16i")], [R("p16f")])
+    cp(T.p15f[:], T.p15i[:], [R("p15i")], [R("p15f")])
+    ts(T.idf[:], T.iom[:], T.iop[:], None, EQ, None, [R("iom"), R("iop")], [R("idf")])
+    if nq:
+        act(T.idb[:], T.idf[:], ACT.Copy, [R("idf")], [R("idb")])
+        ts(T.tg[:], T.iom[:], T.iop[:], None, GT, None, [R("iom"), R("iop")], [R("tg")])
+        ts(T.id128[:], T.idf[:], 128.0, None, MUL, None, [R("idf")], [R("id128")])
+        ts(T.mm[:], T.im32[:], 112, None, AluOpType.bitwise_and, None, [R("im32")], [R("mm")])
+        ts(T.mg[:], T.mm[:], T.p16f[:], None, EQ, None, [R("mm"), R("p16f")], [R("mg")])
+        tt(T.tg[:], T.tg[:], T.mg[:], MUL, [R("tg"), R("mg")], [R("tg")])
+        tt(T.id128[:], T.id128[:], T.tg[:], SUB, [R("id128"), R("tg")], [R("id128")])
+        act(T.wa[:], T.id128[:], ACT.Copy, [R("id128")], [R("wa")])
+        tt(T.mg[:], T.mg[:], T.id128[:], ADD, [R("mg"), R("id128")], [R("mg")])
+        ts(T.wb[:], T.mg[:], -1.0, None, MUL, None, [R("mg")], [R("wb")])
+    cp(T.rf[:], T.ri[:], [R("ri")], [R("rf")])
+    ts(T.rcol[:], T.rf[:], T.p16f[:], None, ADD, None, [R("rf"), R("p16f")], [R("rcol")])
+    for b in range(2):
+        lo, hi = 128 * b, 128 * b + 128
+        ts(T.roh[:, lo:hi], T.iom[:], T.rcol[:, b:b + 1], None, EQ, None, [R("iom"), R("rcol")], [R("roh", lo, hi)])
+    for b in range(2):
+        lo, hi = 128 * b, 128 * b + 128
+        op("T", lambda e: e.transpose(ps(7, lo, hi), T.roh[:, lo:hi], T.idf[:]), [R("roh", lo, hi), R("idf")], (), [7])
+    if nq:
+        act(T.srb[:], ps(7, 0, 256), ACT.Copy, (), [R("srb")], [7])
+    act(T.sr[:], ps(7, 0, 256), ACT.Copy, (), [R("sr")], [7])
+    if nq:
+        order("G", [R("srb")], (), (), ())
+        to_later(lambda k: T.srb[:], T.srl[:, 256 * r:256 * r + 256], "sra", "lss")
+        ts(T.xi[:], T.xi[:], T.p15f[:], None, ADD, None, [R("xi"), R("p15f")], [R("xi")])
+    WC = BLK + BW * (9 - r)
+    iota("win", [[0, Z]], 0, 0, 0, Z)
+    if r == 0:
+        iota("win", [[0, 1]], 0, 0, Z, Z + 1)
+        iota("win", [[0, 1]], 0, 0, Z + V, Z + V + 1)
+    iota("win", [[0, WC - BLK]], 0, 0, BLK, WC)
+    ts(T.selx[:], T.iosx[:], T.iop[:], None, EQ, None, [R("iosx"), R("iop")], [R("selx")])
+
+    def convert():
+        for k in range(CHUNKS):
+            lo, hi = k * CW, (k + 1) * CW
+            cp(T.E0[:, lo:hi], T.ei[:, lo:hi], [R("ei", lo, hi)], [R("E0", lo, hi)])
+
+    for n in range(RO):
+        E, X = ("E0", "E1") if n % 2 == 0 else ("E1", "E0")
+        tw = (1, 0)
+        if n:
+            for i in range(16):
+                op("T", lambda e: e.matmul(T.ps0[:, i:256:16], T[E][:, i:V:16], T.selx[:], True, True), [R(E), R("selx")], (), [0])
+        for b in range(2):
+            lo, hi = 128 * b, 128 * b + 128
+            if n:
+                ts(T.xs[:, lo:hi], ps(0, lo, hi), -1023.75, None, ADD, None, (), [R("xs", lo, hi)], [0])
+            else:
+                ts(T.xs[:, lo:hi], T.xw[:, lo:hi], -1023.75, None, ADD, None, [R("xw", lo, hi)], [R("xs", lo, hi)])
+        for b in range(2):
+            lo, hi = 128 * b, 128 * b + 128
+            op("T", lambda e: e.transpose(ps(tw[b], 256, 384), T.xs[:, lo:hi], T.idf[:]), [R("xs", lo, hi), R("idf")], (), [tw[b]])
+        for b in range(2):
+            lo, hi = 128 * b, 128 * b + 128
+            ts(T.qb[:, lo:hi], ps(tw[b], 256, 384), ROUND_C, ROUND_C, ADD, SUB, (), [R("qb", lo, hi)], [tw[b]])
+        if nq:
+            na = min(4, nq)
+            for b in range(2):
+                oh, sc = "oh%d" % b, "sc%d" % b
+                for k, q in enumerate(later):
+                    ts(T[oh][:, k * SEG + 1:(k + 1) * SEG], T.qb[:, 128 * b:128 * b + 128], float(V * q), None, EQ, None,
+                       [R("qb", 128 * b, 128 * b + 128)], [R(oh, k * SEG + 1, (k + 1) * SEG)])
+                op("V", lambda e: e.tensor_tensor_scan(T[sc][:, 0:nq * SEG], T.d0[:, 0:nq * SEG], T[oh][:, 0:nq * SEG], 0.0, MUL, ADD),
+                   [R(oh), R("d0")], [R(sc)])
+            ts(T.rqv[:], T.qb[:], 1.0 / 16, float(V - 1 - CAP * (r + 1)), MUL, ADD, [R("qb")], [R("rqv")])
+            for b in range(2):
+                sc = "sc%d" % b
+                for k in range(nq):
+                    bk, lo = 2 + 2 * b + k // 4, (k % 4) * CAP
+                    op("T", lambda e: e.matmul(ps(bk, lo, lo + CAP), T.wa[:], T[sc][:, k * SEG + 1:(k + 1) * SEG], True, False), [R(sc), R("wa")], (), [bk])
+                    op("T", lambda e: e.matmul(ps(bk, lo, lo + CAP), T.wb[:], T[sc][:, k * SEG:(k + 1) * SEG - 1], False, True), [R(sc), R("wb")], (), [bk])
+            for b in range(2):
+                for lo, hi, bk in ((0, na * CAP, 2 + 2 * b), (na * CAP, nq * CAP, 3 + 2 * b)):
+                    if hi > lo:
+                        act(T["rl%d" % b][:, lo:hi], ps(bk, 0, hi - lo), ACT.Relu, (), [R("rl%d" % b, lo, hi)], [bk])
+            for b in range(2):
+                rl = "rl%d" % b
+                for k in range(nq):
+                    op("T", lambda e: e.matmul(ps(6 + b, 0, CAP), T.idb[:], T[rl][:, k * CAP:(k + 1) * CAP], k == 0, k == nq - 1),
+                       [R(rl, k * CAP, (k + 1) * CAP), R("idb")], (), [6 + b])
+            if n == 0:
+                convert()
+            for b in range(2):
+                lo, hi, zb = 128 * b, 128 * b + 128, 2 + 2 * b
+                ts(T.yv[:, lo:hi], ps(6 + b, 0, CAP), 4096.0, -float(Z), MUL, ADD, (), [R("yv", lo, hi)], [6 + b])
+                tt(ps(zb, 0, CAP), ps(6 + b, 0, CAP), T.rqv[:, lo:hi], ADD, [R("rqv")], [R("ps%d" % zb)], [6 + b, zb])
+                tt(ps(zb, 0, CAP), ps(zb, 0, CAP), T.yv[:, lo:hi], MIN, [R("yv", lo, hi), R("ps%d" % zb)], [R("ps%d" % zb)], [zb])
+                tt(T.zv[:, lo:hi], ps(zb, 0, CAP), T.xi[:], MAX, [R("xi"), R("ps%d" % zb)], [R("zv", lo, hi)], [zb])
+                cp(T.o16[:, lo:hi], T.zv[:, lo:hi], [R("zv", lo, hi)], [R("o16", lo, hi)])
+            LH = V + CAP * nq
+            act(T.wl0[:, 0:LH].indirect(T.o16[:, 0:128]), T[E][:], ACT.Silu, [R(E), R("o16", 0, 128)], [R("wl0", 0, LH)])
+            cp(T.wl1[:, 0:LH].indirect(T.o16[:, 128:256]), T[E][:], [R(E), R("o16", 128, 256)], [R("wl1", 0, LH)])
+            before = [("lsq", total["lsq"])] if n else []
+            for b in range(2):
+                wl, items = "wl%d" % b, []
+                for k in range(nq):
+                    lo = V + CAP * k
+                    items.append((T.rqb[k, b::2, :], T[wl][b::16, lo:lo + CAP], [R(wl, lo, lo + CAP)], ()))
+                tok = dmas("S" if b == 0 else "Y", "dq%d" % b, items, before)
+                need("G", tok[0], tok[1])
+            to_later(lambda k: T.rqb[k], T.rland[r], "rq%d" % r, "lsq")
+        elif n == 0:
+            convert()
+        for b in range(2):
+            for k in range(4):
+                bk, lo = 2 + k, 512 * k
+                op("T", lambda e: e.matmul(ps(bk, 0, 512), T.sr[:, 128 * b:128 * b + 128], T[E][:, lo:lo + 512], True, True), [R("sr"), R(E, lo, lo + 512)], (), [bk])
+                s = 1 if (k == 0 and r == 0) else 0
+                c0 = Z + V * b + lo
+                act(T.win[:, c0 + s:c0 + 512], ps(bk, s, 512), ACT.Copy, (), [R("win", c0 + s, c0 + 512)], [bk])
+        for b in range(2):
+            lo, hi = 128 * b, 128 * b + 128
+            ts(T.u1[:, lo:hi], T.qb[:, lo:hi], 8.0, 1023.75 - V * r - 8.0 * V * r + Z + V * b + Z, MUL, ADD, [R("qb", lo, hi)], [R("u1", lo, hi)])
+            ts(T.a1[:, lo:hi], T.qb[:, lo:hi], BW / 2048.0, float(BLK + Z + b - BW * r), MUL, ADD, [R("qb", lo, hi)], [R("a1", lo, hi)])
+            tt(T.u1[:, lo:hi], ps(tw[b], 256, 384), T.u1[:, lo:hi], ADD, [R("u1", lo, hi)], [R("u1", lo, hi)], [tw[b]])
+        tt(T.u1[:], T.u1[:], T.a1[:], MIN, [R("u1"), R("a1")], [R("u1")])
+        if nq:
+            for b in range(2):
+                lo, hi = 128 * b, 128 * b + 128
+                ts(T.si[:, lo:hi], ps(6 + b, 0, CAP), -1.0, 129.0, ADD, MUL, (), [R("si", lo, hi)], [6 + b])
+            ts(T.si[:], T.si[:], 3, 254, AluOpType.arith_shift_right, AluOpType.bitwise_and, [R("si")], [R("si")])
+            tt(T.av[:], T.yv[:], T.si[:], MIN, [R("yv"), R("si")], [R("av")])
+            tt(T.av[:], T.av[:], T.u1[:], ADD, [R("av"), R("u1")], [R("av")])
+        else:
+            ts(T.av[:], T.u1[:], -float(Z), None, ADD, None, [R("u1")], [R("av")])
+        cp(T.a16[:], T.av[:], [R("av")], [R("a16")])
+        if n == 0 and nr:
+            got = tokens("sra", sum(width(topo, cores, p) for p in range(nr)))
+            cp(T.srf[:, 0:256 * nr], T.srl[:, 0:256 * nr], (), [R("srf", 0, 256 * nr)], (), [got])
+
+        def gather(p):
+            c0, c1 = 16 * p, 16 * p + 16
+            arr = tokens("rq%d" % p, width(topo, cores, p))
+            dmas("Y", "lw%d" % p, [(T.lq[:, c0:c1], T.rland[p], (), [R("lq", c0, c1)])], [arr])
+            ts(T.lo[:, c0:c1], T.lq[:, c0:c1], 0.25 - V * r, None, ADD, None, [R("lq", c0, c1)], [R("lo", c0, c1)])
+            cp(T.rpf[:, 16 * c0:16 * c1], T[E][:, 0:V].indirect(T.lo[:, c0:c1]), [R(E), R("lo", c0, c1)], [R("rpf", 16 * c0, 16 * c1)])
+            bk = (0, 1, 6, 7)[p % 4]
+            for b in range(2):
+                m = 256 * p + 128 * b
+                op("T", lambda e: e.matmul(T["ps%d" % bk][:, b:256:2], T.srf[:, m:m + 128], T.rpf[:, 256 * p + b:256 * p + 256:2], True, True),
+                   [R("srf", m, m + 128), R("rpf", 16 * c0, 16 * c1)], (), [bk])
+
+        def reply(p):
+            lo, hi, bk = 256 * p, 256 * p + 256, (0, 1, 6, 7)[p % 4]
+            left = [("ls%d" % p, total["ls%d" % p])] if n else []
+            tok = cp(T.rp[:, lo:hi], ps(bk, 0, 256), (), [R("rp", lo, hi)], [bk], left)
+            need("G", tok[0], tok[1])
+            rid, pid, _s = topo.addr(cores[p])
+            k = r - p - 1
+            g.remote_dma(out_ap=T.ld[:, 256 * k:256 * k + 256], in_ap=T.rp[:, lo:hi], remote_sem=T.sem["rp%d" % r],
+                         local_sem=T.sem["ls%d" % p], pid=pid, routing_id=rid, dma_engine_mask=rem_mask(pool))
+            tokens("ls%d" % p, len(pool))
+        if nr:
+            gather(0)
+            reply(0)
+        for p in range(1, nr + 1):
+            if p < nr:
+                gather(p)
+            if p > 1:
+                reply(p - 1)
+        for k, q in enumerate(later):
+            arr = tokens("rp%d" % q, len(out_engines(topo, cores, q)))
+            c0 = BLK + BW * (k + 1) + Z
+            cp(T.win[:, c0:c0 + 256], T.ld[:, 256 * k:256 * k + 256], (), [R("win", c0, c0 + 256)], (), [arr])
+        op("V", lambda e: e.tensor_tensor(T[X][:], T.win[:, 0:WC].indirect(T.a16[:, 0:128]), T[E][:], MAX), [R("win", 0, WC), R("a16"), R(E)], [R(X)])
+        pieces = 1 if n < RO - 1 else PIECES
+        for k in range(pieces):
+            lo, hi = k * V // pieces, (k + 1) * V // pieces
+            op("V", lambda e: e.tensor_tensor(T[X][:, lo:hi], T.win[:, 0:WC].indirect(T.a16[:, 128 + lo // 16:128 + hi // 16]), T[X][:, lo:hi], MAX),
+               [R("win", 0, WC), R("a16"), R(X, lo, hi)], [R(X, lo, hi)])
+            if n == RO - 1:
+                dmas("Y" if k % 2 == 0 else "S", "st%d" % k, [(T.y[:, lo:hi], T[X][:, lo:hi], [R(X, lo, hi)], ())])
+    for sem in sorted(total):
+        need("G", sem, total[sem])

@@ -3,49 +3,50 @@ from concourse.bass import DstId, RemoteDMATransfer
 from concourse.mybir import AluOpType, ActivationFunctionType
 
 V, N, RO, CAP = 2048, 8, 3, 128
-SEG = CAP + 1
-Z = 8
-BLK = Z + 2 * V
-BW = Z + 2 * CAP
-WCOLS = BLK + 9 * BW
 LCOLS = V + 7 * CAP
+WCOLS = V + 7 * 2 * CAP
 CHUNKS, PIECES = 4, 8
-ROUND_C = 1.5 * 2.0 ** 34
+LOOK = 2
+AHEAD_V, AHEAD_S = 2, 2
+QB = 160
 
 SCRATCH = {
     "ei": ("sbuf", [128, V], "int32"), "E0": ("sbuf", [128, V], "float32"), "E1": ("sbuf", [128, V], "float32"),
-    "xw": ("sbuf", [128, 256], "int32"), "win": ("sbuf", [128, WCOLS], "float32"),
+    "xw": ("sbuf", [128, 256], "int32"), "win": ("sbuf", [128, WCOLS], "float32"), "p1": ("sbuf", [128, V], "float32"),
+    "ab": ("sbuf", [128, V], "float32"),
     "wl0": ("sbuf", [128, LCOLS], "float32"), "wl1": ("sbuf", [128, LCOLS], "float32"),
     "ri": ("sbuf", [128, 2], "int32"), "rf": ("sbuf", [128, 2], "float32"), "rcol": ("sbuf", [128, 2], "float32"),
     "iom": ("sbuf", [128, 128], "float32"), "iop": ("sbuf", [128, 1], "float32"), "iosx": ("sbuf", [128, 16], "float32"),
     "ip32": ("sbuf", [128, 1], "int32"), "im32": ("sbuf", [128, 128], "int32"),
     "p16i": ("sbuf", [128, 1], "int32"), "p15i": ("sbuf", [128, 1], "int32"),
     "p16f": ("sbuf", [128, 1], "float32"), "p15f": ("sbuf", [128, 1], "float32"),
+    "cq": ("sbuf", [128, 1], "float32"), "cr": ("sbuf", [128, 1], "float32"),
     "mm": ("sbuf", [128, 128], "int32"), "mg": ("sbuf", [128, 128], "float32"), "tg": ("sbuf", [128, 128], "float32"),
     "idf": ("sbuf", [128, 128], "float32"), "id128": ("sbuf", [128, 128], "float32"), "selx": ("sbuf", [128, 16], "float32"),
-    "idb": ("sbuf", [128, 128], "bfloat16"), "wa": ("sbuf", [128, 128], "bfloat16"), "wb": ("sbuf", [128, 128], "bfloat16"),
-    "xi": ("sbuf", [128, 128], "float32"), "d0": ("sbuf", [128, 7 * SEG], "bfloat16"),
-    "oh0": ("sbuf", [128, 7 * SEG], "bfloat16"), "oh1": ("sbuf", [128, 7 * SEG], "bfloat16"),
-    "sc0": ("sbuf", [128, 7 * SEG], "bfloat16"), "sc1": ("sbuf", [128, 7 * SEG], "bfloat16"),
-    "rl0": ("sbuf", [128, 7 * CAP], "bfloat16"), "rl1": ("sbuf", [128, 7 * CAP], "bfloat16"),
+    "idb": ("sbuf", [128, 128], "bfloat16"), "id7": ("sbuf", [128, 128], "bfloat16"), "id19": ("sbuf", [128, 128], "bfloat16"),
+    "wo": ("sbuf", [128, 128], "bfloat16"), "ws": ("sbuf", [128, 128], "bfloat16"),
+    "xa": ("sbuf", [128, 256], "bfloat16"), "xb": ("sbuf", [128, 256], "bfloat16"), "d0": ("sbuf", [128, 512], "bfloat16"),
+    "oh": ("sbuf", [128, 7 * 256], "bfloat16"), "sc": ("sbuf", [128, 7 * 256], "bfloat16"), "rl": ("sbuf", [128, 7 * 256], "bfloat16"),
     "roh": ("sbuf", [128, 256], "float32"), "sr": ("sbuf", [128, 256], "float32"), "srb": ("sbuf", [128, 256], "bfloat16"),
     "srl": ("sbuf", [128, 7 * 256], "bfloat16"), "srf": ("sbuf", [128, 7 * 256], "float32"),
-    "xs": ("sbuf", [128, 256], "float32"), "qb": ("sbuf", [128, 256], "bfloat16"), "rqv": ("sbuf", [128, 256], "float32"),
-    "yv": ("sbuf", [128, 256], "float32"), "zv": ("sbuf", [128, 256], "float32"), "o16": ("sbuf", [128, 256], "uint16"),
-    "u1": ("sbuf", [128, 256], "float32"), "a1": ("sbuf", [128, 256], "float32"),
-    "si": ("sbuf", [128, 256], "int32"), "av": ("sbuf", [128, 256], "float32"), "a16": ("sbuf", [128, 256], "uint16"),
+    "xs": ("sbuf", [128, 256], "float32"), "qt": ("sbuf", [128, 256], "bfloat16"), "kq": ("sbuf", [128, 256], "bfloat16"),
+    "own": ("sbuf", [128, 256], "bfloat16"), "lf": ("sbuf", [128, 256], "float32"), "l16": ("sbuf", [128, 256], "uint16"),
+    "zv": ("sbuf", [128, 256], "float32"), "o16": ("sbuf", [128, 256], "uint16"),
+    "gi": ("sbuf", [128, 128], "int32"), "si": ("sbuf", [128, 128], "int32"), "rb": ("sbuf", [128, 128], "float32"), "yv": ("sbuf", [128, 128], "float32"),
+    "av": ("sbuf", [128, 128], "float32"), "a16": ("sbuf", [128, 128], "uint16"),
+    "cs": ("sbuf", [128, 8], "float32"), "cs16": ("sbuf", [128, 8], "uint16"),
     "lq": ("sbuf", [128, 7 * 16], "float32"), "lo": ("sbuf", [128, 7 * 16], "uint16"), "rpf": ("sbuf", [128, 7 * 256], "float32"),
     "rp": ("sbuf", [128, 7 * 256], "uint16"), "ld": ("sbuf", [128, 7 * 256], "uint16"),
     "rqb": ("dram", [7, 128, 16], "float32"), "rland": ("dram", [7, 128, 16], "float32"),
 }
 for _k in range(8):
-    SCRATCH["ps%d" % _k] = ("psum", [128, 512], "float32")
-SEMAPHORES = (["qV", "qT", "qS", "qG", "lri", "lx0", "lx1", "dq0", "dq1", "lsq", "lss", "sra"]
+    SCRATCH["ps%d" % _k] = ("psum", [128, 1024], "bfloat16") if _k == 1 else ("psum", [128, 512], "float32")
+SEMAPHORES = (["qV", "qT", "qS", "qG", "lri", "lx0", "lx1", "dq0", "dq1", "lsq", "lss", "sra", "srh"]
               + ["le%d" % k for k in range(CHUNKS)] + ["st%d" % k for k in range(PIECES)]
               + ["rq%d" % k for k in range(7)] + ["rp%d" % k for k in range(8)] + ["ls%d" % k for k in range(7)] + ["lw%d" % k for k in range(7)])
 
-ADD, SUB, MUL, MAX, MIN, EQ, GT = (AluOpType.add, AluOpType.subtract, AluOpType.mult, AluOpType.max, AluOpType.min,
-                                   AluOpType.is_equal, AluOpType.is_gt)
+ADD, SUB, MUL, MAX, MIN, EQ, LE = (AluOpType.add, AluOpType.subtract, AluOpType.mult, AluOpType.max, AluOpType.min,
+                                   AluOpType.is_equal, AluOpType.is_le)
 ACT = ActivationFunctionType
 
 
@@ -54,11 +55,34 @@ def out_engines(topo, cores, q):
     return topo.engines(cores[q], far[0])
 
 
-def width(topo, cores, p):
-    n, w = len(out_engines(topo, cores, p)), 1
-    while 2 * w * max(N - 1 - p, 1) <= n:
-        w *= 2
-    return w
+def deal(engs, n):
+    w = [1] * n
+    while sum(w) + min(w) <= len(engs):
+        w[w.index(min(w))] *= 2
+    return [engs[sum(w[:k]):sum(w[:k + 1])] for k in range(n)]
+
+
+def on_chip(topo, cores, q):
+    return [p for p in range(N) if topo.chip(cores[p]) == topo.chip(cores[q])]
+
+
+def matrix_dests(topo, cores, p):
+    return [q for q in range(p + 1, N) if q in on_chip(topo, cores, p) or q == on_chip(topo, cores, q)[-1]]
+
+
+def reply_engines(topo, cores, q, p):
+    pool = out_engines(topo, cores, q)
+    if p in on_chip(topo, cores, q) and on_chip(topo, cores, q)[0] > 0:
+        return [e for e in topo.engines(cores[q], cores[p]) if e not in pool]
+    return pool
+
+
+def serve_order(topo, cores, q):
+    return sorted(range(q), key=lambda p: (p in on_chip(topo, cores, q), on_chip(topo, cores, p).index(p), p))
+
+
+def stages(n):
+    return ([1] if n % 2 == 0 else []) + [2] * ((n - 1) // 2) + [1] if n else []
 
 
 def rank_program(g, core, T, topo):
@@ -155,14 +179,23 @@ def rank_program(g, core, T, topo):
 
     pool = out_engines(topo, cores, r)
 
-    def to_later(src, dst, remote, local):
-        w, transfers = width(topo, cores, r), []
-        for k, q in enumerate(later):
+    def fan_out(dests, src, dst, remote, local):
+        transfers = []
+        for k, (q, engs) in enumerate(zip(dests, deal(pool, len(dests)))):
             rid, pid, _s = topo.addr(cores[q])
-            transfers.append(RemoteDMATransfer(dst_ids=[DstId(rid=rid, pnc=pid)], dma_engine_mask=rem_mask(pool[k * w:(k + 1) * w]),
+            transfers.append(RemoteDMATransfer(dst_ids=[DstId(rid=rid, pnc=pid)], dma_engine_mask=rem_mask(engs),
                                                remote_sem=T.sem[remote], src=src(k), dst=dst, alu_op=0))
+            tokens(local, len(engs))
         g.remote_dma_fused(transfers, local_sem=T.sem[local])
-        tokens(local, w * nq)
+
+    def width(p, dests):
+        return len(deal(out_engines(topo, cores, p), len(dests))[dests.index(r)])
+
+    def send(q, src, dst, remote, local, engs):
+        rid, pid, _s = topo.addr(cores[q])
+        g.remote_dma(out_ap=dst, in_ap=src, remote_sem=T.sem[remote], local_sem=T.sem[local], pid=pid, routing_id=rid,
+                     dma_engine_mask=rem_mask(engs))
+        tokens(local, len(engs))
 
     CW = V // CHUNKS
     dmas("S", "lri", [(T.ri[:], T.rights[:], (), [R("ri")])])
@@ -180,10 +213,10 @@ def rank_program(g, core, T, topo):
         else:
             op("G", lambda e: e.iota(T[name][:, lo:hi], pat, base, cm), (), [(name, lo, hi)])
 
-    def ts(out, i, s1, s2, op0, op1, reads, writes, banks=(), q="V"):
+    def ts(out, i, s1, s2, op0, op1, reads, writes, banks=(), extra=()):
         if op1 is None:
-            return op(q, lambda e: e.tensor_scalar(out, i, s1, None, op0), reads, writes, banks)
-        return op(q, lambda e: e.tensor_scalar(out, i, s1, s2, op0, op1), reads, writes, banks)
+            return op("V", lambda e: e.tensor_scalar(out, i, s1, None, op0), reads, writes, banks, extra)
+        return op("V", lambda e: e.tensor_scalar(out, i, s1, s2, op0, op1), reads, writes, banks, extra)
 
     def tt(out, i0, i1, o, reads, writes, banks=()):
         return op("V", lambda e: e.tensor_tensor(out, i0, i1, o), reads, writes, banks)
@@ -191,42 +224,48 @@ def rank_program(g, core, T, topo):
     def cp(out, i, reads, writes, banks=(), extra=()):
         return op("V", lambda e: e.tensor_copy(out, i), reads, writes, banks, extra)
 
-    def act(out, i, f, reads, writes, banks=()):
-        return op("S", lambda e: e.activation(out, i, f), reads, writes, banks)
+    def act(out, i, f, reads, writes, banks=(), extra=(), **kw):
+        return op("S", lambda e: e.activation(out, i, f, **kw), reads, writes, banks, extra)
+
+    def mm(out, lhs, rhs, start, stop, reads, bk):
+        return op("T", lambda e: e.matmul(out, lhs, rhs, start, stop), reads, (), [bk])
 
     def mset(ap, val, wr):
         op("V", lambda e: e.memset(ap, val), (), [wr])
 
+    LH, WH = V + CAP * nq, V + 2 * CAP * nq
     iota("iop", [[1, 1]], 0, 1, 0, 1)
     iota("ip32", [[1, 1]], 0, 1, 0, 1, False)
     iota("iom", [[1, 128]], 0, 0, 0, 128)
     if nq:
-        mset(T.d0[:], 1.0, R("d0"))
-        mset(T.oh0[:, 0:7 * SEG:SEG], 0.0, R("oh0"))
-        mset(T.oh1[:, 0:7 * SEG:SEG], 0.0, R("oh1"))
-        mset(T.d0[:, 0:7 * SEG:SEG], 0.0, R("d0"))
         iota("im32", [[1, 128]], 0, 0, 0, 128, False)
-        iota("xi", [[16, 128]], 0, 0, 0, 128)
+        iota("xa", [[0, 2], [16, 128]], 0, 0, 0, 256)
+        mset(T.d0[:], 1.0, R("d0"))
+        mset(T.d0[:, 0:512:CAP], 0.0, R("d0"))
+        for lo in range(V, LH, 512):
+            hi = min(lo + 512, LH)
+            act(T.wl0[:, lo:hi], T.d0[:, 0:hi - lo], ACT.Silu, [R("d0")], [R("wl0", lo, hi)])
+            act(T.wl1[:, lo:hi], T.d0[:, 0:hi - lo], ACT.Copy, [R("d0")], [R("wl1", lo, hi)])
     iota("iosx", [[1, 2], [16, 8]], 0, 0, 0, 16)
-    if nq:
-        for b in range(2):
-            iota("wl%d" % b, [[V, nq], [0, CAP]], V * (r + 1), 0, V, V + CAP * nq)
+    iota("win", [[0, 1]], 0, 0, 0, 1)
+    iota("p1", [[0, 1]], 0, 0, 0, 1)
     ts(T.p16i[:], T.ip32[:], 112, None, AluOpType.bitwise_and, None, [R("ip32")], [R("p16i")])
     ts(T.p15i[:], T.ip32[:], 15, None, AluOpType.bitwise_and, None, [R("ip32")], [R("p15i")])
     cp(T.p16f[:], T.p16i[:], [R("p16i")], [R("p16f")])
     cp(T.p15f[:], T.p15i[:], [R("p15i")], [R("p15f")])
     ts(T.idf[:], T.iom[:], T.iop[:], None, EQ, None, [R("iom"), R("iop")], [R("idf")])
+    act(T.idb[:], T.idf[:], ACT.Copy, [R("idf")], [R("idb")])
     if nq:
-        act(T.idb[:], T.idf[:], ACT.Copy, [R("idf")], [R("idb")])
-        ts(T.tg[:], T.iom[:], T.iop[:], None, GT, None, [R("iom"), R("iop")], [R("tg")])
-        ts(T.id128[:], T.idf[:], 128.0, None, MUL, None, [R("idf")], [R("id128")])
+        act(T.id19[:], T.idf[:], ACT.Copy, [R("idf")], [R("id19")], scale=2.0 ** -19)
+        act(T.id7[:], T.idf[:], ACT.Copy, [R("idf")], [R("id7")], scale=2.0 ** -7)
+        act(T.xb[:], T.xa[:], ACT.Identity, [R("xa"), R("p15f")], [R("xb")], bias=T.p15f[:], scale=0.0)
         ts(T.mm[:], T.im32[:], 112, None, AluOpType.bitwise_and, None, [R("im32")], [R("mm")])
         ts(T.mg[:], T.mm[:], T.p16f[:], None, EQ, None, [R("mm"), R("p16f")], [R("mg")])
+        act(T.ws[:], T.mg[:], ACT.Copy, [R("mg")], [R("ws")], scale=-1.0)
+        ts(T.tg[:], T.iom[:], T.iop[:], None, LE, None, [R("iom"), R("iop")], [R("tg")])
+        ts(T.id128[:], T.idf[:], 128.0, None, MUL, None, [R("idf")], [R("id128")])
         tt(T.tg[:], T.tg[:], T.mg[:], MUL, [R("tg"), R("mg")], [R("tg")])
-        tt(T.id128[:], T.id128[:], T.tg[:], SUB, [R("id128"), R("tg")], [R("id128")])
-        act(T.wa[:], T.id128[:], ACT.Copy, [R("id128")], [R("wa")])
-        tt(T.mg[:], T.mg[:], T.id128[:], ADD, [R("mg"), R("id128")], [R("mg")])
-        ts(T.wb[:], T.mg[:], -1.0, None, MUL, None, [R("mg")], [R("wb")])
+        tt(T.wo[:], T.id128[:], T.tg[:], ADD, [R("id128"), R("tg")], [R("wo")])
     cp(T.rf[:], T.ri[:], [R("ri")], [R("rf")])
     ts(T.rcol[:], T.rf[:], T.p16f[:], None, ADD, None, [R("rf"), R("p16f")], [R("rcol")])
     for b in range(2):
@@ -234,82 +273,86 @@ def rank_program(g, core, T, topo):
         ts(T.roh[:, lo:hi], T.iom[:], T.rcol[:, b:b + 1], None, EQ, None, [R("iom"), R("rcol")], [R("roh", lo, hi)])
     for b in range(2):
         lo, hi = 128 * b, 128 * b + 128
-        op("T", lambda e: e.transpose(ps(7, lo, hi), T.roh[:, lo:hi], T.idf[:]), [R("roh", lo, hi), R("idf")], (), [7])
+        op("T", lambda e: e.transpose(ps(0, lo, hi), T.roh[:, lo:hi], T.idf[:]), [R("roh", lo, hi), R("idf")], (), [0])
     if nq:
-        act(T.srb[:], ps(7, 0, 256), ACT.Copy, (), [R("srb")], [7])
-    act(T.sr[:], ps(7, 0, 256), ACT.Copy, (), [R("sr")], [7])
+        act(T.srb[:], ps(0, 0, 256), ACT.Copy, (), [R("srb")], [0])
+    act(T.sr[:], ps(0, 0, 256), ACT.Copy, (), [R("sr")], [0])
     if nq:
         order("G", [R("srb")], (), (), ())
-        to_later(lambda k: T.srb[:], T.srl[:, 256 * r:256 * r + 256], "sra", "lss")
-        ts(T.xi[:], T.xi[:], T.p15f[:], None, ADD, None, [R("xi"), R("p15f")], [R("xi")])
-    WC = BLK + BW * (9 - r)
-    iota("win", [[0, Z]], 0, 0, 0, Z)
-    if r == 0:
-        iota("win", [[0, 1]], 0, 0, Z, Z + 1)
-        iota("win", [[0, 1]], 0, 0, Z + V, Z + V + 1)
-    iota("win", [[0, WC - BLK]], 0, 0, BLK, WC)
-    ts(T.selx[:], T.iosx[:], T.iop[:], None, EQ, None, [R("iosx"), R("iop")], [R("selx")])
+        fan_out(matrix_dests(topo, cores, r), lambda k: T.srb[:], T.srl[:, 256 * r:256 * r + 256], "sra", "lss")
+    mates = on_chip(topo, cores, r)
+    senders = [p for p in range(nr) if r in matrix_dests(topo, cores, p)]
+    got = [tokens("sra", sum(width(p, matrix_dests(topo, cores, p)) for p in senders))] if senders else []
+    if mates[0] and r == mates[-1]:
+        need("G", got[0][0], got[0][1])
+        for q in mates[:-1]:
+            send(q, T.srl[:, 0:256 * mates[0]], T.srl[:, 0:256 * mates[0]], "srh", "lss", topo.engines(core, cores[q]))
+    elif mates[0]:
+        got.append(tokens("srh", len(topo.engines(cores[mates[-1]], core))))
 
-    def convert():
-        for k in range(CHUNKS):
-            lo, hi = k * CW, (k + 1) * CW
-            cp(T.E0[:, lo:hi], T.ei[:, lo:hi], [R("ei", lo, hi)], [R("E0", lo, hi)])
+    def late_constants():
+        ts(T.selx[:], T.iosx[:], T.iop[:], None, EQ, None, [R("iosx"), R("iop")], [R("selx")])
+        mset(T.cq[:], QB - 0.5 + 0.25 / V, R("cq"))
+        mset(T.cr[:], -float(V * r), R("cr"))
+        if nq:
+            ts(T.cs[:], T.iom[:, 0:8], 0.125, T.p15f[:], MUL, ADD, [R("iom"), R("p15f")], [R("cs")])
+            ts(T.cs16[:], T.cs[:], 8.0, None, MUL, None, [R("cs")], [R("cs16")])
 
+    PW = V // PIECES
+    served, free = serve_order(topo, cores, r), (7, 6, 0)
     for n in range(RO):
         E, X = ("E0", "E1") if n % 2 == 0 else ("E1", "E0")
-        tw = (1, 0)
+        last = n == RO - 1
         if n:
             for i in range(16):
-                op("T", lambda e: e.matmul(T.ps0[:, i:256:16], T[E][:, i:V:16], T.selx[:], True, True), [R(E), R("selx")], (), [0])
+                mm(T.ps0[:, i:256:16], T[E][:, i:V:16], T.selx[:], True, True, [R(E), R("selx")], 0)
+            act(T.qt[:], ps(0, 0, 256), ACT.Identity, [R("cq")], [R("qt")], [0], bias=T.cq[:], scale=1.0 / V)
+            act(T.xs[:], ps(0, 0, 256), ACT.Identity, [R("cr")], [R("xs")], [0], bias=T.cr[:])
+        else:
+            ts(T.qt[:], T.xw[:], 1.0 / V, QB - 0.5 + 0.25 / V, MUL, ADD, [R("xw")], [R("qt")])
         for b in range(2):
             lo, hi = 128 * b, 128 * b + 128
-            if n:
-                ts(T.xs[:, lo:hi], ps(0, lo, hi), -1023.75, None, ADD, None, (), [R("xs", lo, hi)], [0])
-            else:
-                ts(T.xs[:, lo:hi], T.xw[:, lo:hi], -1023.75, None, ADD, None, [R("xw", lo, hi)], [R("xs", lo, hi)])
-        for b in range(2):
-            lo, hi = 128 * b, 128 * b + 128
-            op("T", lambda e: e.transpose(ps(tw[b], 256, 384), T.xs[:, lo:hi], T.idf[:]), [R("xs", lo, hi), R("idf")], (), [tw[b]])
-        for b in range(2):
-            lo, hi = 128 * b, 128 * b + 128
-            ts(T.qb[:, lo:hi], ps(tw[b], 256, 384), ROUND_C, ROUND_C, ADD, SUB, (), [R("qb", lo, hi)], [tw[b]])
+            op("T", lambda e: e.transpose(ps(1, lo, hi), T.qt[:, lo:hi], T.idb[:]), [R("qt"), R("idb")], (), [1])
         if nq:
-            na = min(4, nq)
-            for b in range(2):
-                oh, sc = "oh%d" % b, "sc%d" % b
-                for k, q in enumerate(later):
-                    ts(T[oh][:, k * SEG + 1:(k + 1) * SEG], T.qb[:, 128 * b:128 * b + 128], float(V * q), None, EQ, None,
-                       [R("qb", 128 * b, 128 * b + 128)], [R(oh, k * SEG + 1, (k + 1) * SEG)])
-                op("V", lambda e: e.tensor_tensor_scan(T[sc][:, 0:nq * SEG], T.d0[:, 0:nq * SEG], T[oh][:, 0:nq * SEG], 0.0, MUL, ADD),
-                   [R(oh), R("d0")], [R(sc)])
-            ts(T.rqv[:], T.qb[:], 1.0 / 16, float(V - 1 - CAP * (r + 1)), MUL, ADD, [R("qb")], [R("rqv")])
-            for b in range(2):
-                sc = "sc%d" % b
-                for k in range(nq):
-                    bk, lo = 2 + 2 * b + k // 4, (k % 4) * CAP
-                    op("T", lambda e: e.matmul(ps(bk, lo, lo + CAP), T.wa[:], T[sc][:, k * SEG + 1:(k + 1) * SEG], True, False), [R(sc), R("wa")], (), [bk])
-                    op("T", lambda e: e.matmul(ps(bk, lo, lo + CAP), T.wb[:], T[sc][:, k * SEG:(k + 1) * SEG - 1], False, True), [R(sc), R("wb")], (), [bk])
-            for b in range(2):
-                for lo, hi, bk in ((0, na * CAP, 2 + 2 * b), (na * CAP, nq * CAP, 3 + 2 * b)):
-                    if hi > lo:
-                        act(T["rl%d" % b][:, lo:hi], ps(bk, 0, hi - lo), ACT.Relu, (), [R("rl%d" % b, lo, hi)], [bk])
-            for b in range(2):
-                rl = "rl%d" % b
-                for k in range(nq):
-                    op("T", lambda e: e.matmul(ps(6 + b, 0, CAP), T.idb[:], T[rl][:, k * CAP:(k + 1) * CAP], k == 0, k == nq - 1),
-                       [R(rl, k * CAP, (k + 1) * CAP), R("idb")], (), [6 + b])
-            if n == 0:
-                convert()
-            for b in range(2):
-                lo, hi, zb = 128 * b, 128 * b + 128, 2 + 2 * b
-                ts(T.yv[:, lo:hi], ps(6 + b, 0, CAP), 4096.0, -float(Z), MUL, ADD, (), [R("yv", lo, hi)], [6 + b])
-                tt(ps(zb, 0, CAP), ps(6 + b, 0, CAP), T.rqv[:, lo:hi], ADD, [R("rqv")], [R("ps%d" % zb)], [6 + b, zb])
-                tt(ps(zb, 0, CAP), ps(zb, 0, CAP), T.yv[:, lo:hi], MIN, [R("yv", lo, hi), R("ps%d" % zb)], [R("ps%d" % zb)], [zb])
-                tt(T.zv[:, lo:hi], ps(zb, 0, CAP), T.xi[:], MAX, [R("xi"), R("ps%d" % zb)], [R("zv", lo, hi)], [zb])
-                cp(T.o16[:, lo:hi], T.zv[:, lo:hi], [R("zv", lo, hi)], [R("o16", lo, hi)])
-            LH = V + CAP * nq
-            act(T.wl0[:, 0:LH].indirect(T.o16[:, 0:128]), T[E][:], ACT.Silu, [R(E), R("o16", 0, 128)], [R("wl0", 0, LH)])
-            cp(T.wl1[:, 0:LH].indirect(T.o16[:, 128:256]), T[E][:], [R(E), R("o16", 128, 256)], [R("wl1", 0, LH)])
+            mm(ps(6, 0, 256), T.id19[:], T.xa[:], True, False, [R("id19"), R("xa")], 6)
+            mm(ps(6, 0, 256), T.id19[:], T.xb[:], False, False, [R("id19"), R("xb")], 6)
+
+        def sums(k0, k1):
+            for k in range(k0, k1):
+                lo, hi = 256 * k, 256 * k + 256
+                mm(ps(6, 0, 256), T.id7[:], T.rl[:, lo:hi], False, k == nq - 1, [R("rl", lo, hi), R("id7")], 6)
+        k0, prev = 0, None
+        for s, w in enumerate(stages(nq)):
+            lo, hi, bk = 256 * k0, 256 * (k0 + w), 2 + s
+            for k in range(k0, k0 + w):
+                ts(T.oh[:, 256 * k:256 * k + 256], ps(1, 0, 256), float(QB + later[k]), None, EQ, None, (), [R("oh", 256 * k, 256 * k + 256)], [1])
+            op("V", lambda e: e.tensor_tensor_scan(T.sc[:, lo:hi], T.d0[:, 0:hi - lo], T.oh[:, lo:hi], 0.0, MUL, ADD),
+               [R("oh", lo, hi), R("d0")], [R("sc", lo, hi)])
+            mm(ps(bk, 0, hi - lo), T.wo[:], T.oh[:, lo:hi], True, False, [R("oh", lo, hi), R("wo")], bk)
+            mm(ps(bk, 0, hi - lo), T.ws[:], T.sc[:, lo:hi], False, True, [R("sc", lo, hi), R("ws")], bk)
+            act(T.rl[:, lo:hi], ps(bk, 0, hi - lo), ACT.Relu, (), [R("rl", lo, hi)], [bk])
+            if prev:
+                sums(*prev)
+            prev, k0 = (k0, k0 + w), k0 + w
+        if nq:
+            sums(*prev)
+            ts(T.kq[:], ps(1, 0, 256), -float(QB + r + 1), 0.0, ADD, MAX, (), [R("kq")], [1])
+
+        def own():
+            ts(T.own[:], ps(1, 0, 256), float(QB + r), None, EQ, None, (), [R("own")], [1])
+        if n:
+            own()
+        else:
+            for k in range(CHUNKS):
+                lo, hi = k * CW, (k + 1) * CW
+                cp(T.E0[:, lo:hi], T.ei[:, lo:hi], [R("ei", lo, hi)], [R("E0", lo, hi)])
+        if nq:
+            ts(ps(7, 0, 256), ps(6, 0, 256), 4096.0, (1 - V) / CAP, MUL, ADD, (), [R("ps7")], [6, 7])
+            tt(T.zv[:], ps(6, 0, 256), T.kq[:], ADD, [R("kq")], [R("zv")], [6])
+            tt(T.zv[:], ps(7, 0, 256), T.zv[:], MIN, [R("zv"), R("ps7")], [R("zv")], [7])
+            ts(T.o16[:], T.zv[:], float(CAP), float(V - 1), MUL, ADD, [R("zv")], [R("o16")])
+            act(T.wl0[:, 0:LH].indirect(T.o16[:, 0:128]), T[E][:], ACT.Silu, [R(E), R("o16")], [R("wl0", 0, LH)])
+            cp(T.wl1[:, 0:LH].indirect(T.o16[:, 128:256]), T[E][:], [R(E), R("o16")], [R("wl1", 0, LH)])
             before = [("lsq", total["lsq"])] if n else []
             for b in range(2):
                 wl, items = "wl%d" % b, []
@@ -318,77 +361,119 @@ def rank_program(g, core, T, topo):
                     items.append((T.rqb[k, b::2, :], T[wl][b::16, lo:lo + CAP], [R(wl, lo, lo + CAP)], ()))
                 tok = dmas("S" if b == 0 else "Y", "dq%d" % b, items, before)
                 need("G", tok[0], tok[1])
-            to_later(lambda k: T.rqb[k], T.rland[r], "rq%d" % r, "lsq")
-        elif n == 0:
-            convert()
-        for b in range(2):
-            for k in range(4):
-                bk, lo = 2 + k, 512 * k
-                op("T", lambda e: e.matmul(ps(bk, 0, 512), T.sr[:, 128 * b:128 * b + 128], T[E][:, lo:lo + 512], True, True), [R("sr"), R(E, lo, lo + 512)], (), [bk])
-                s = 1 if (k == 0 and r == 0) else 0
-                c0 = Z + V * b + lo
-                act(T.win[:, c0 + s:c0 + 512], ps(bk, s, 512), ACT.Copy, (), [R("win", c0 + s, c0 + 512)], [bk])
-        for b in range(2):
-            lo, hi = 128 * b, 128 * b + 128
-            ts(T.u1[:, lo:hi], T.qb[:, lo:hi], 8.0, 1023.75 - V * r - 8.0 * V * r + Z + V * b + Z, MUL, ADD, [R("qb", lo, hi)], [R("u1", lo, hi)])
-            ts(T.a1[:, lo:hi], T.qb[:, lo:hi], BW / 2048.0, float(BLK + Z + b - BW * r), MUL, ADD, [R("qb", lo, hi)], [R("a1", lo, hi)])
-            tt(T.u1[:, lo:hi], ps(tw[b], 256, 384), T.u1[:, lo:hi], ADD, [R("u1", lo, hi)], [R("u1", lo, hi)], [tw[b]])
-        tt(T.u1[:], T.u1[:], T.a1[:], MIN, [R("u1"), R("a1")], [R("u1")])
-        if nq:
+            fan_out(later, lambda k: T.rqb[k], T.rland[r], "rq%d" % r, "lsq")
+        if n == 0:
+            ts(T.xs[:], T.xw[:], -float(V * r), None, ADD, None, [R("xw")], [R("xs")])
+            own()
+
+        def turn():
             for b in range(2):
                 lo, hi = 128 * b, 128 * b + 128
-                ts(T.si[:, lo:hi], ps(6 + b, 0, CAP), -1.0, 129.0, ADD, MUL, (), [R("si", lo, hi)], [6 + b])
-            ts(T.si[:], T.si[:], 3, 254, AluOpType.arith_shift_right, AluOpType.bitwise_and, [R("si")], [R("si")])
-            tt(T.av[:], T.yv[:], T.si[:], MIN, [R("yv"), R("si")], [R("av")])
-            tt(T.av[:], T.av[:], T.u1[:], ADD, [R("av"), R("u1")], [R("av")])
-        else:
-            ts(T.av[:], T.u1[:], -float(Z), None, ADD, None, [R("u1")], [R("av")])
-        cp(T.a16[:], T.av[:], [R("av")], [R("a16")])
+                op("T", lambda e: e.transpose(ps(0, 256 + lo, 256 + hi), T.xs[:, lo:hi], T.idf[:]), [R("xs"), R("idf")], (), [0])
+
+        def permute(b, name, k0, k1):
+            for k in range(k0, k1):
+                bk, lo = 2 + k, 512 * k
+                mm(ps(bk, 0, 512), T.sr[:, 128 * b:128 * b + 128], T[E][:, lo:lo + 512], True, True, [R("sr"), R(E, lo, lo + 512)], bk)
+                s = 1 if k == 0 else 0
+                act(T[name][:, lo + s:lo + 512], ps(bk, s, 512), ACT.Copy, (), [R(name, lo + s, lo + 512)], [bk])
+        if n:
+            turn()
+        permute(1, "p1", 0, 4)
+        if n == 0:
+            turn()
+        ahead_s = AHEAD_S if nq and nr else 4
+        permute(0, "win", 0, ahead_s)
         if n == 0 and nr:
-            got = tokens("sra", sum(width(topo, cores, p) for p in range(nr)))
-            cp(T.srf[:, 0:256 * nr], T.srl[:, 0:256 * nr], (), [R("srf", 0, 256 * nr)], (), [got])
+            act(T.srf[:, 0:256 * nr], T.srl[:, 0:256 * nr], ACT.Copy, (), [R("srf", 0, 256 * nr)], (), got)
+        tt(T.lf[:], ps(0, 256, 512), T.own[:], MUL, [R("own")], [R("lf")], [0])
+        cp(T.l16[:], T.lf[:], [R("lf")], [R("l16")])
+        if nq:
+            ts(T.gi[:], ps(6, 0, CAP), float(CAP), None, MUL, None, (), [R("gi")], [6])
+            ts(T.si[:], T.gi[:], -1.0, 129.0, ADD, MUL, [R("gi")], [R("si")])
+            ts(T.yv[:], T.gi[:], 4096.0, None, MUL, None, [R("gi")], [R("yv")])
+            ts(T.si[:], T.si[:], 4, 127, AluOpType.arith_shift_right, AluOpType.bitwise_and, [R("si")], [R("si")])
+            ts(T.rb[:], T.kq[:, 0:CAP], 2.0 * CAP, float(V), MUL, ADD, [R("kq")], [R("rb")])
+            tt(T.av[:], T.si[:], T.rb[:], ADD, [R("si"), R("rb")], [R("av")])
+            tt(T.av[:], T.av[:], T.yv[:], MIN, [R("av"), R("yv")], [R("av")])
+            tt(T.av[:], T.av[:], T.lf[:, 0:CAP], MAX, [R("av"), R("lf")], [R("av")])
+            cp(T.a16[:], T.av[:], [R("av")], [R("a16")])
+        if n == 0:
+            late_constants()
+
+        def store(k):
+            lo, hi = k * PW, (k + 1) * PW
+            dmas("Y", "st%d" % k, [(T.y[:, lo:hi], T[X][:, lo:hi], [R(X, lo, hi)], ())])
+
+        M = "wl1" if nq else X
+
+        def local(k):
+            lo, hi = k * PW, (k + 1) * PW
+            tt(T[M][:, lo:hi], T.p1[:, 0:V].indirect(T.l16[:, CAP + lo // 16:CAP + hi // 16]), T[E][:, lo:hi], MAX,
+               [R("p1"), R("l16"), R(E, lo, hi)], [R(M, lo, hi)])
+        ahead = AHEAD_V if nq and nr else PIECES
+        for k in range(ahead):
+            local(k)
+        if not nq:
+            for k in range(PIECES):
+                lo, hi = k * PW, (k + 1) * PW
+                tt(T[X][:, lo:hi], T.win[:, 0:V].indirect(T.l16[:, lo // 16:hi // 16]), T[X][:, lo:hi], MAX,
+                   [R("win", 0, V), R("l16"), R(X, lo, hi)], [R(X, lo, hi)])
+                if last:
+                    store(k)
 
         def gather(p):
             c0, c1 = 16 * p, 16 * p + 16
-            arr = tokens("rq%d" % p, width(topo, cores, p))
+            arr = tokens("rq%d" % p, width(p, list(range(p + 1, N))))
             dmas("Y", "lw%d" % p, [(T.lq[:, c0:c1], T.rland[p], (), [R("lq", c0, c1)])], [arr])
-            ts(T.lo[:, c0:c1], T.lq[:, c0:c1], 0.25 - V * r, None, ADD, None, [R("lq", c0, c1)], [R("lo", c0, c1)])
-            cp(T.rpf[:, 16 * c0:16 * c1], T[E][:, 0:V].indirect(T.lo[:, c0:c1]), [R(E), R("lo", c0, c1)], [R("rpf", 16 * c0, 16 * c1)])
-            bk = (0, 1, 6, 7)[p % 4]
+            ts(T.lo[:, c0:c1], T.lq[:, c0:c1], 0.25 - V * r, float(V - 1), ADD, MIN, [R("lq", c0, c1)], [R("lo", c0, c1)])
+            act(T.rpf[:, 16 * c0:16 * c1], T[E][:, 0:V].indirect(T.lo[:, c0:c1]), ACT.Copy, [R(E), R("lo", c0, c1)], [R("rpf", 16 * c0, 16 * c1)])
+            bk = free[served.index(p) % len(free)]
             for b in range(2):
                 m = 256 * p + 128 * b
-                op("T", lambda e: e.matmul(T["ps%d" % bk][:, b:256:2], T.srf[:, m:m + 128], T.rpf[:, 256 * p + b:256 * p + 256:2], True, True),
-                   [R("srf", m, m + 128), R("rpf", 16 * c0, 16 * c1)], (), [bk])
+                mm(ps(bk, 128 * b, 128 * b + 128), T.srf[:, m:m + 128], T.rpf[:, 256 * p + b:256 * p + 256:2], True, True,
+                   [R("srf", m, m + 128), R("rpf", 16 * c0, 16 * c1)], bk)
 
         def reply(p):
-            lo, hi, bk = 256 * p, 256 * p + 256, (0, 1, 6, 7)[p % 4]
+            lo, hi, bk = 256 * p, 256 * p + 256, free[served.index(p) % len(free)]
             left = [("ls%d" % p, total["ls%d" % p])] if n else []
             tok = cp(T.rp[:, lo:hi], ps(bk, 0, 256), (), [R("rp", lo, hi)], [bk], left)
             need("G", tok[0], tok[1])
-            rid, pid, _s = topo.addr(cores[p])
             k = r - p - 1
-            g.remote_dma(out_ap=T.ld[:, 256 * k:256 * k + 256], in_ap=T.rp[:, lo:hi], remote_sem=T.sem["rp%d" % r],
-                         local_sem=T.sem["ls%d" % p], pid=pid, routing_id=rid, dma_engine_mask=rem_mask(pool))
-            tokens("ls%d" % p, len(pool))
-        if nr:
-            gather(0)
-            reply(0)
-        for p in range(1, nr + 1):
-            if p < nr:
-                gather(p)
-            if p > 1:
-                reply(p - 1)
-        for k, q in enumerate(later):
-            arr = tokens("rp%d" % q, len(out_engines(topo, cores, q)))
-            c0 = BLK + BW * (k + 1) + Z
+            send(p, T.rp[:, lo:hi], T.ld[:, 256 * k:256 * k + 256], "rp%d" % r, "ls%d" % p, reply_engines(topo, cores, r, p))
+        for j in range(nr + LOOK):
+            if j < nr:
+                gather(served[j])
+            if 0 <= j - LOOK:
+                reply(served[j - LOOK])
+        permute(0, "win", ahead_s, 4)
+        for k in range(ahead, PIECES):
+            local(k)
+        if not nq:
+            continue
+        def land(k):
+            arr = tokens("rp%d" % later[k], len(reply_engines(topo, cores, later[k], r)))
+            c0 = V + 256 * k
             cp(T.win[:, c0:c0 + 256], T.ld[:, 256 * k:256 * k + 256], (), [R("win", c0, c0 + 256)], (), [arr])
-        op("V", lambda e: e.tensor_tensor(T[X][:], T.win[:, 0:WC].indirect(T.a16[:, 0:128]), T[E][:], MAX), [R("win", 0, WC), R("a16"), R(E)], [R(X)])
-        pieces = 1 if n < RO - 1 else PIECES
-        for k in range(pieces):
-            lo, hi = k * V // pieces, (k + 1) * V // pieces
-            op("V", lambda e: e.tensor_tensor(T[X][:, lo:hi], T.win[:, 0:WC].indirect(T.a16[:, 128 + lo // 16:128 + hi // 16]), T[X][:, lo:hi], MAX),
-               [R("win", 0, WC), R("a16"), R(X, lo, hi)], [R(X, lo, hi)])
-            if n == RO - 1:
-                dmas("Y" if k % 2 == 0 else "S", "st%d" % k, [(T.y[:, lo:hi], T[X][:, lo:hi], [R(X, lo, hi)], ())])
+
+        def fold(k):
+            c0, s0 = V + 256 * k, V + CAP * k
+            tt(T.wl1[:, s0:s0 + CAP], T.win[:, c0 + CAP:c0 + 256].indirect(T.cs16[:]), T.wl1[:, s0:s0 + CAP], MAX,
+               [R("win", c0 + CAP, c0 + 256), R("cs16"), R("wl1", s0, s0 + CAP)], [R("wl1", s0, s0 + CAP)])
+        ks = sorted(range(nq), key=lambda k: serve_order(topo, cores, later[k]).index(r))
+        for k in ks[:-2]:
+            land(k)
+            fold(k)
+        for k in ks[-2:]:
+            land(k)
+        for k in ks[-2:]:
+            fold(k)
+        for k in range(PIECES):
+            lo, hi = k * PW, (k + 1) * PW
+            act(T.ab[:, lo:hi], T.win[:, 0:WH].indirect(T.a16[:, lo // 16:hi // 16]), ACT.Copy, [R("win", 0, WH), R("a16")], [R("ab", lo, hi)])
+            tt(T[X][:, lo:hi], T.wl1[:, 0:LH].indirect(T.o16[:, CAP + lo // 16:CAP + hi // 16]), T.ab[:, lo:hi], MAX,
+               [R("wl1", 0, LH), R("o16"), R("ab", lo, hi)], [R(X, lo, hi)])
+            if last:
+                store(k)
     for sem in sorted(total):
         need("G", sem, total[sem])

@@ -1,14 +1,17 @@
 import numpy as np
-from concourse.bass import DstId, RemoteDMATransfer
+from concourse.bass import DstId, IndirectOffsetOnAxis, RemoteDMATransfer
 from concourse.mybir import AluOpType, ActivationFunctionType
 
-V, N, RO, CAP = 2048, 8, 3, 128
-LCOLS = V + 7 * CAP
+V, N, RO, CAP, ALL = 2048, 8, 3, 128, 128
+LCOLS = V + 8 + 8 * CAP
 WCOLS = V + 7 * 2 * CAP
 CHUNKS, PIECES = 4, 8
 LOOK = 2
-AHEAD_V, AHEAD_S = 2, 2
+AHEAD_V, AHEAD_S = 1, 4
+DIRECT = 4
+QUARTERS = True
 QB = 160
+HALF = -0.5 + 0.25 / V
 
 SCRATCH = {
     "ei": ("sbuf", [128, V], "int32"), "E0": ("sbuf", [128, V], "float32"), "E1": ("sbuf", [128, V], "float32"),
@@ -16,37 +19,44 @@ SCRATCH = {
     "ab": ("sbuf", [128, V], "float32"),
     "wl0": ("sbuf", [128, LCOLS], "float32"), "wl1": ("sbuf", [128, LCOLS], "float32"),
     "ri": ("sbuf", [128, 2], "int32"), "rf": ("sbuf", [128, 2], "float32"), "rcol": ("sbuf", [128, 2], "float32"),
-    "iom": ("sbuf", [128, 128], "float32"), "iop": ("sbuf", [128, 1], "float32"), "iosx": ("sbuf", [128, 16], "float32"),
+    "iom": ("sbuf", [128, 128], "float32"), "iop": ("sbuf", [128, 1], "float32"), "qb": ("sbuf", [128, 256], "bfloat16"),
+    "hm": ("sbuf", [128, 128], "bfloat16"), "hc": ("sbuf", [128, 512], "bfloat16"),
+    "q4f": ("sbuf", [128, 32], "float32"), "q4b": ("sbuf", [128, 32], "bfloat16"),
     "ip32": ("sbuf", [128, 1], "int32"), "im32": ("sbuf", [128, 128], "int32"),
     "p16i": ("sbuf", [128, 1], "int32"), "p15i": ("sbuf", [128, 1], "int32"),
     "p16f": ("sbuf", [128, 1], "float32"), "p15f": ("sbuf", [128, 1], "float32"),
     "cq": ("sbuf", [128, 1], "float32"), "cr": ("sbuf", [128, 1], "float32"),
     "mm": ("sbuf", [128, 128], "int32"), "mg": ("sbuf", [128, 128], "float32"), "tg": ("sbuf", [128, 128], "float32"),
-    "idf": ("sbuf", [128, 128], "float32"), "id128": ("sbuf", [128, 128], "float32"), "selx": ("sbuf", [128, 16], "float32"),
-    "idb": ("sbuf", [128, 128], "bfloat16"), "id7": ("sbuf", [128, 128], "bfloat16"), "id19": ("sbuf", [128, 128], "bfloat16"),
+    "idf": ("sbuf", [128, 128], "float32"), "id128": ("sbuf", [128, 128], "float32"), "selx": ("sbuf", [128, 64], "float32"),
+    "idb": ("sbuf", [128, 128], "bfloat16"), "idg": ("sbuf", [128, 128], "bfloat16"), "idx": ("sbuf", [128, 128], "bfloat16"),
     "wo": ("sbuf", [128, 128], "bfloat16"), "ws": ("sbuf", [128, 128], "bfloat16"),
     "xa": ("sbuf", [128, 256], "bfloat16"), "xb": ("sbuf", [128, 256], "bfloat16"), "d0": ("sbuf", [128, 512], "bfloat16"),
     "oh": ("sbuf", [128, 7 * 256], "bfloat16"), "sc": ("sbuf", [128, 7 * 256], "bfloat16"), "rl": ("sbuf", [128, 7 * 256], "bfloat16"),
-    "roh": ("sbuf", [128, 256], "float32"), "sr": ("sbuf", [128, 256], "float32"), "srb": ("sbuf", [128, 256], "bfloat16"),
-    "srl": ("sbuf", [128, 7 * 256], "bfloat16"), "srf": ("sbuf", [128, 7 * 256], "float32"),
-    "xs": ("sbuf", [128, 256], "float32"), "qt": ("sbuf", [128, 256], "bfloat16"), "kq": ("sbuf", [128, 256], "bfloat16"),
+    "roh": ("sbuf", [128, 256], "float32"), "sr": ("sbuf", [128, 128], "float32"), "srb": ("sbuf", [128, 256], "bfloat16"),
+    "co": ("sbuf", [128, 2], "float32"), "co16": ("sbuf", [128, 2], "uint16"), "sm": ("sbuf", [128, 32], "bfloat16"),
+    "ex": ("sbuf", [128, 7 * 16], "float32"), "ex16": ("sbuf", [128, 7 * 16], "uint16"),
+    "srl": ("sbuf", [128, 16 + 7 * 32], "bfloat16"), "srf": ("sbuf", [128, 7 * 256], "float32"),
+    "xs": ("sbuf", [128, 1024], "float32"), "qt": ("sbuf", [128, 1024], "bfloat16"), "kq": ("sbuf", [128, 256], "bfloat16"),
     "own": ("sbuf", [128, 256], "bfloat16"), "lf": ("sbuf", [128, 256], "float32"), "l16": ("sbuf", [128, 256], "uint16"),
     "zv": ("sbuf", [128, 256], "float32"), "o16": ("sbuf", [128, 256], "uint16"),
-    "gi": ("sbuf", [128, 128], "int32"), "si": ("sbuf", [128, 128], "int32"), "rb": ("sbuf", [128, 128], "float32"), "yv": ("sbuf", [128, 128], "float32"),
-    "av": ("sbuf", [128, 128], "float32"), "a16": ("sbuf", [128, 128], "uint16"),
-    "cs": ("sbuf", [128, 8], "float32"), "cs16": ("sbuf", [128, 8], "uint16"),
-    "lq": ("sbuf", [128, 7 * 16], "float32"), "lo": ("sbuf", [128, 7 * 16], "uint16"), "rpf": ("sbuf", [128, 7 * 256], "float32"),
+    "gi": ("sbuf", [128, 128], "int32"), "si": ("sbuf", [128, 128], "int32"), "rb": ("sbuf", [128, 128], "float32"),
+    "yv": ("sbuf", [128, 128], "float32"), "av": ("sbuf", [128, 128], "float32"), "a16": ("sbuf", [128, 128], "uint16"),
+    "cs": ("sbuf", [128, 8], "float32"), "cs16": ("sbuf", [128, 8], "uint16"), "ro16": ("sbuf", [128, 8], "uint16"),
+    "lw": ("sbuf", [128, 128], "float32"), "lr": ("sbuf", [128, 7 * 16], "float32"), "cv": ("sbuf", [128, 7 * 16], "float32"),
+    "lq": ("sbuf", [128, 7 * 16], "uint16"), "lo": ("sbuf", [128, 7 * 16], "uint16"), "rpf": ("sbuf", [128, 7 * 256], "float32"),
     "rp": ("sbuf", [128, 7 * 256], "uint16"), "ld": ("sbuf", [128, 7 * 256], "uint16"),
-    "rqb": ("dram", [7, 128, 16], "float32"), "rland": ("dram", [7, 128, 16], "float32"),
+    "ll": ("sbuf", [128, 7 * 16], "float32"), "rqb": ("dram", [7, 128, 16], "float32"), "rland": ("dram", [7, 128, 16], "float32"),
+    "ed": ("dram", [128, V], "float32"), "pi": ("sbuf", [128, V], "int32"), "rix": ("sbuf", [128, 1], "int32"),
 }
 for _k in range(8):
-    SCRATCH["ps%d" % _k] = ("psum", [128, 1024], "bfloat16") if _k == 1 else ("psum", [128, 512], "float32")
+    SCRATCH["ps%d" % _k] = ("psum", [128, 512], "float32")
 SEMAPHORES = (["qV", "qT", "qS", "qG", "lri", "lx0", "lx1", "dq0", "dq1", "lsq", "lss", "sra", "srh"]
               + ["le%d" % k for k in range(CHUNKS)] + ["st%d" % k for k in range(PIECES)]
-              + ["rq%d" % k for k in range(7)] + ["rp%d" % k for k in range(8)] + ["ls%d" % k for k in range(7)] + ["lw%d" % k for k in range(7)])
+              + ["rq%d" % k for k in range(7)] + ["rp%d" % k for k in range(8)] + ["ls%d" % k for k in range(7)]
+              + ["lw%d" % k for k in range(7)] + ["ig", "hi0", "hi1"])
 
-ADD, SUB, MUL, MAX, MIN, EQ, LE = (AluOpType.add, AluOpType.subtract, AluOpType.mult, AluOpType.max, AluOpType.min,
-                                   AluOpType.is_equal, AluOpType.is_le)
+ADD, MUL, MAX, MIN, EQ, LE, GE = (AluOpType.add, AluOpType.mult, AluOpType.max, AluOpType.min,
+                                  AluOpType.is_equal, AluOpType.is_le, AluOpType.is_ge)
 ACT = ActivationFunctionType
 
 
@@ -67,18 +77,101 @@ def on_chip(topo, cores, q):
 
 
 def matrix_dests(topo, cores, p):
-    return [q for q in range(p + 1, N) if q in on_chip(topo, cores, p) or q == on_chip(topo, cores, q)[-1]]
+    out = []
+    for q in range(p + 1, N):
+        there = on_chip(topo, cores, q)
+        if p in there:
+            out.append(cores[q])
+        elif q == there[-1]:
+            out.append(relay(topo, cores, there[on_chip(topo, cores, p).index(p)], p) or cores[q])
+    return out
 
 
 def reply_engines(topo, cores, q, p):
-    pool = out_engines(topo, cores, q)
-    if p in on_chip(topo, cores, q) and on_chip(topo, cores, q)[0] > 0:
-        return [e for e in topo.engines(cores[q], cores[p]) if e not in pool]
+    pool, h = out_engines(topo, cores, q), relay(topo, cores, q, p)
+    to = cores[p] if h is None else h
+    if topo.chip(to) == topo.chip(cores[q]) and on_chip(topo, cores, q)[0] > 0:
+        return [e for e in topo.engines(cores[q], to) if e not in pool]
     return pool
+
+
+def fan(topo, cores, p, dests):
+    pool = out_engines(topo, cores, p)
+    far = sorted((q for q in dests if topo.chip(q) != topo.chip(cores[p])), reverse=True)
+    near = [q for q in dests if q not in far]
+    if not far:
+        return [list(zip(near, deal(pool, len(near))))]
+    most = len(pool) // 2
+    calls = [list(zip(far[k:k + most], deal(pool, len(far[k:k + most])))) for k in range(0, len(far), most)]
+    for q in near:
+        calls[0].append((q, [e for e in topo.engines(cores[p], q) if e not in pool][:most]))
+    return calls
+
+
+def width(calls, to):
+    return [len(engs) for call in calls for c, engs in call if c == to][0]
+
+
+def direct(topo, cores, p):
+    return sum(q not in on_chip(topo, cores, p) for q in range(p + 1, N)) <= DIRECT
+
+
+def asks(topo, cores, p):
+    later = list(cores[p + 1:])
+    if direct(topo, cores, p):
+        return fan(topo, cores, p, later)
+    return [list(zip(later, deal(out_engines(topo, cores, p), len(later))))]
 
 
 def serve_order(topo, cores, q):
     return sorted(range(q), key=lambda p: (p in on_chip(topo, cores, q), on_chip(topo, cores, p).index(p), p))
+
+
+def relay(topo, cores, q, p):
+    to = topo.chip(cores[p])
+    chips = sorted({topo.chip(c) for c in cores[p + 1:]} - {to}, key=lambda c: (not topo.same_plane(c, to), -c))
+    if topo.chip(cores[q]) == to:
+        return None
+    way = chips.index(topo.chip(cores[q]))
+    if way == 0:
+        return None
+    if way == 1:
+        near = [c for c in topo.cores_of(cores[q]) if topo.die(c) != topo.die(cores[q])]
+    else:
+        near = [c for c in range(ALL) if topo.mates(topo.chip(c), to) and topo.die(c) == topo.die(cores[q])]
+    near = [c for c in near if c not in cores and topo.may_write(c, cores[p]) and topo.may_write(cores[q], c)]
+    return near[on_chip(topo, cores, q).index(q)]
+
+
+def landing_engines(topo, cores, q, p):
+    h = relay(topo, cores, q, p)
+    return reply_engines(topo, cores, q, p) if h is None else topo.engines(h, cores[p])
+
+
+def hand_on(g, core, T, topo):
+    cores, left = T.cores, 0
+    jobs = [(q, p) for q in range(N) for p in serve_order(topo, cores, q) if relay(topo, cores, q, p) == core]
+    for p in range(N):
+        if core in matrix_dests(topo, cores, p):
+            g.wait_ge(T.sem.sra, width(fan(topo, cores, p, matrix_dests(topo, cores, p)), core))
+            there, piece, transfers = on_chip(topo, cores, jobs[0][0]), T.srl[:, 16 + 32 * p:48 + 32 * p], []
+            for q, engs in zip(there, deal(topo.engines(core, cores[p]), len(there))):
+                rid, pid, _s = topo.addr(cores[q])
+                transfers.append(RemoteDMATransfer(dst_ids=[DstId(rid=rid, pnc=pid)], dma_engine_mask=sum(1 << e for e in engs),
+                                                   remote_sem=T.sem.srh, src=piece, dst=piece, alu_op=0))
+                left += len(engs)
+            g.remote_dma_fused(transfers, local_sem=T.sem.lss)
+    for n in range(RO):
+        for q, p in jobs:
+            j, k, engs = on_chip(topo, cores, p).index(p), q - p - 1, topo.engines(core, cores[p])
+            g.wait_ge(T.sem["hi%d" % j], (n + 1) * len(reply_engines(topo, cores, q, p)))
+            rid, pid, _s = topo.addr(cores[p])
+            c0 = 256 * (2 * n + j)
+            g.remote_dma(out_ap=T.ld[:, 256 * k:256 * k + 256], in_ap=T.rp[:, c0:c0 + 256], remote_sem=T.sem["rp%d" % q],
+                         local_sem=T.sem.lss, pid=pid, routing_id=rid, dma_engine_mask=sum(1 << e for e in engs))
+            left += len(engs)
+    if left:
+        g.wait_ge(T.sem.lss, left)
 
 
 def stages(n):
@@ -88,7 +181,7 @@ def stages(n):
 def rank_program(g, core, T, topo):
     r = T.rank_of(core)
     if r is None:
-        return
+        return hand_on(g, core, T, topo)
     cores = T.cores
     later = list(range(r + 1, N))
     nq, nr = len(later), r
@@ -175,24 +268,19 @@ def rank_program(g, core, T, topo):
         return m
 
     def R(name, lo=0, hi=1 << 20):
-        return (name, lo, min(hi, SCRATCH[name][1][-1]))
+        return (name, lo, min(hi, SCRATCH[name][1][-1]) if name in SCRATCH else hi)
 
-    pool = out_engines(topo, cores, r)
-
-    def fan_out(dests, src, dst, remote, local):
+    def fan_out(call, src, dst, remote, local):
         transfers = []
-        for k, (q, engs) in enumerate(zip(dests, deal(pool, len(dests)))):
-            rid, pid, _s = topo.addr(cores[q])
+        for c, engs in call:
+            rid, pid, _s = topo.addr(c)
             transfers.append(RemoteDMATransfer(dst_ids=[DstId(rid=rid, pnc=pid)], dma_engine_mask=rem_mask(engs),
-                                               remote_sem=T.sem[remote], src=src(k), dst=dst, alu_op=0))
+                                               remote_sem=T.sem[remote], src=src(T.rank_of(c)), dst=dst, alu_op=0))
             tokens(local, len(engs))
         g.remote_dma_fused(transfers, local_sem=T.sem[local])
 
-    def width(p, dests):
-        return len(deal(out_engines(topo, cores, p), len(dests))[dests.index(r)])
-
-    def send(q, src, dst, remote, local, engs):
-        rid, pid, _s = topo.addr(cores[q])
+    def send(to, src, dst, remote, local, engs):
+        rid, pid, _s = topo.addr(to)
         g.remote_dma(out_ap=dst, in_ap=src, remote_sem=T.sem[remote], local_sem=T.sem[local], pid=pid, routing_id=rid,
                      dma_engine_mask=rem_mask(engs))
         tokens(local, len(engs))
@@ -233,7 +321,12 @@ def rank_program(g, core, T, topo):
     def mset(ap, val, wr):
         op("V", lambda e: e.memset(ap, val), (), [wr])
 
-    LH, WH = V + CAP * nq, V + 2 * CAP * nq
+    if direct(topo, cores, r):
+        ST = 1 << max(nq - 1, 0).bit_length()
+        GW, F, L0 = float(ST), 1.0, V - 1 + ST
+    else:
+        ST, GW, F, L0 = nq, 1.0 / CAP, float(CAP), V
+    LH, WH = L0 + CAP * ST, V + 2 * CAP * nq
     iota("iop", [[1, 1]], 0, 1, 0, 1)
     iota("ip32", [[1, 1]], 0, 1, 0, 1, False)
     iota("iom", [[1, 128]], 0, 0, 0, 128)
@@ -242,13 +335,7 @@ def rank_program(g, core, T, topo):
         iota("xa", [[0, 2], [16, 128]], 0, 0, 0, 256)
         mset(T.d0[:], 1.0, R("d0"))
         mset(T.d0[:, 0:512:CAP], 0.0, R("d0"))
-        for lo in range(V, LH, 512):
-            hi = min(lo + 512, LH)
-            act(T.wl0[:, lo:hi], T.d0[:, 0:hi - lo], ACT.Silu, [R("d0")], [R("wl0", lo, hi)])
-            act(T.wl1[:, lo:hi], T.d0[:, 0:hi - lo], ACT.Copy, [R("d0")], [R("wl1", lo, hi)])
-    iota("iosx", [[1, 2], [16, 8]], 0, 0, 0, 16)
     iota("win", [[0, 1]], 0, 0, 0, 1)
-    iota("p1", [[0, 1]], 0, 0, 0, 1)
     ts(T.p16i[:], T.ip32[:], 112, None, AluOpType.bitwise_and, None, [R("ip32")], [R("p16i")])
     ts(T.p15i[:], T.ip32[:], 15, None, AluOpType.bitwise_and, None, [R("ip32")], [R("p15i")])
     cp(T.p16f[:], T.p16i[:], [R("p16i")], [R("p16f")])
@@ -256,47 +343,111 @@ def rank_program(g, core, T, topo):
     ts(T.idf[:], T.iom[:], T.iop[:], None, EQ, None, [R("iom"), R("iop")], [R("idf")])
     act(T.idb[:], T.idf[:], ACT.Copy, [R("idf")], [R("idb")])
     if nq:
-        act(T.id19[:], T.idf[:], ACT.Copy, [R("idf")], [R("id19")], scale=2.0 ** -19)
-        act(T.id7[:], T.idf[:], ACT.Copy, [R("idf")], [R("id7")], scale=2.0 ** -7)
-        act(T.xb[:], T.xa[:], ACT.Identity, [R("xa"), R("p15f")], [R("xb")], bias=T.p15f[:], scale=0.0)
         ts(T.mm[:], T.im32[:], 112, None, AluOpType.bitwise_and, None, [R("im32")], [R("mm")])
-        ts(T.mg[:], T.mm[:], T.p16f[:], None, EQ, None, [R("mm"), R("p16f")], [R("mg")])
-        act(T.ws[:], T.mg[:], ACT.Copy, [R("mg")], [R("ws")], scale=-1.0)
         ts(T.tg[:], T.iom[:], T.iop[:], None, LE, None, [R("iom"), R("iop")], [R("tg")])
-        ts(T.id128[:], T.idf[:], 128.0, None, MUL, None, [R("idf")], [R("id128")])
-        tt(T.tg[:], T.tg[:], T.mg[:], MUL, [R("tg"), R("mg")], [R("tg")])
-        tt(T.wo[:], T.id128[:], T.tg[:], ADD, [R("id128"), R("tg")], [R("wo")])
+        ts(T.mg[:], T.mm[:], T.p16f[:], None, EQ, None, [R("mm"), R("p16f")], [R("mg")])
     cp(T.rf[:], T.ri[:], [R("ri")], [R("rf")])
+    if nq:
+        ts(T.id128[:], T.idf[:], 128.0, None, MUL, None, [R("idf")], [R("id128")])
     ts(T.rcol[:], T.rf[:], T.p16f[:], None, ADD, None, [R("rf"), R("p16f")], [R("rcol")])
+    if nq:
+        iota("co", [[128, 2]], 0, 1, 0, 2)
+        cp(T.co16[:], T.co[:], [R("co")], [R("co16")])
     for b in range(2):
         lo, hi = 128 * b, 128 * b + 128
         ts(T.roh[:, lo:hi], T.iom[:], T.rcol[:, b:b + 1], None, EQ, None, [R("iom"), R("rcol")], [R("roh", lo, hi)])
     for b in range(2):
         lo, hi = 128 * b, 128 * b + 128
-        op("T", lambda e: e.transpose(ps(0, lo, hi), T.roh[:, lo:hi], T.idf[:]), [R("roh", lo, hi), R("idf")], (), [0])
+        op("T", lambda e: e.transpose(ps(3, lo, hi), T.roh[:, lo:hi], T.idf[:]), [R("roh", lo, hi), R("idf")], (), [3])
     if nq:
-        act(T.srb[:], ps(0, 0, 256), ACT.Copy, (), [R("srb")], [0])
-    act(T.sr[:], ps(0, 0, 256), ACT.Copy, (), [R("sr")], [0])
+        act(T.idx[:], T.idf[:], ACT.Copy, [R("idf")], [R("idx")], scale=GW * 2.0 ** -15)
+        act(T.xb[:], T.xa[:], ACT.Identity, [R("xa"), R("p15f")], [R("xb")], bias=T.p15f[:], scale=0.0)
+        act(T.srb[:], ps(3, 0, 256), ACT.Copy, (), [R("srb")], [3])
+        act(T.sm[:], T.srb[:].indirect(T.co16[:]), ACT.Copy, [R("srb"), R("co16")], [R("sm")])
+        act(T.ws[:], T.mg[:], ACT.Copy, [R("mg")], [R("ws")], scale=-1.0)
+        act(T.idg[:], T.idf[:], ACT.Copy, [R("idf")], [R("idg")], scale=GW)
+        tt(T.tg[:], T.tg[:], T.mg[:], MUL, [R("tg"), R("mg")], [R("tg")])
+    cp(T.rix[:], T.rcol[:, 1:2], [R("rcol")], [R("rix")])
     if nq:
-        order("G", [R("srb")], (), (), ())
-        fan_out(matrix_dests(topo, cores, r), lambda k: T.srb[:], T.srl[:, 256 * r:256 * r + 256], "sra", "lss")
-    mates = on_chip(topo, cores, r)
-    senders = [p for p in range(nr) if r in matrix_dests(topo, cores, p)]
-    got = [tokens("sra", sum(width(p, matrix_dests(topo, cores, p)) for p in senders))] if senders else []
-    if mates[0] and r == mates[-1]:
-        need("G", got[0][0], got[0][1])
-        for q in mates[:-1]:
-            send(q, T.srl[:, 0:256 * mates[0]], T.srl[:, 0:256 * mates[0]], "srh", "lss", topo.engines(core, cores[q]))
-    elif mates[0]:
-        got.append(tokens("srh", len(topo.engines(cores[mates[-1]], core))))
+        tt(T.wo[:], T.id128[:], T.tg[:], ADD, [R("id128"), R("tg")], [R("wo")])
+        for lo in range(V, LH, 512):
+            hi = min(lo + 512, LH)
+            act(T.wl0[:, lo:hi], T.d0[:, 0:hi - lo], ACT.Silu, [R("d0")], [R("wl0", lo, hi)])
+        order("G", [R("sm")], (), (), ())
+        for call in fan(topo, cores, r, matrix_dests(topo, cores, r)):
+            fan_out(call, lambda q: T.sm[:], T.srl[:, 16 + 32 * r:48 + 32 * r], "sra", "lss")
 
-    def late_constants():
-        ts(T.selx[:], T.iosx[:], T.iop[:], None, EQ, None, [R("iosx"), R("iop")], [R("selx")])
-        mset(T.cq[:], QB - 0.5 + 0.25 / V, R("cq"))
-        mset(T.cr[:], -float(V * r), R("cr"))
-        if nq:
-            ts(T.cs[:], T.iom[:, 0:8], 0.125, T.p15f[:], MUL, ADD, [R("iom"), R("p15f")], [R("cs")])
-            ts(T.cs16[:], T.cs[:], 8.0, None, MUL, None, [R("cs")], [R("cs16")])
+    def rows(name, src):
+        reads, writes = [R("rix"), (src, 0, V)], [R(name)]
+        order("G", reads, writes, (), ())
+        g.indirect_dma_start(T[name][:], None, T[src][:], IndirectOffsetOnAxis(ap=T.rix[:], axis=0), bounds_check=127).then_inc(T.sem.ig, 16)
+        note("G", tokens("ig", 16), reads, writes, ())
+    rows("pi", "ends")
+    ts(T.qt[:, 0:256], T.xw[:], 1.0 / V, QB + HALF, MUL, ADD, [R("xw")], [R("qt", 0, 256)])
+    if nq:
+        iota("wl1", [[0, LH - V]], 0, 0, V, LH)
+        if F == 1:
+            iota("cv", [[-V, nq], [0, 16]], -V * (r + 1), 0, 0, 16 * nq)
+    mset(T.cq[:], HALF - 3.0 * QB if QUARTERS else HALF + QB, R("cq"))
+    mset(T.cr[:], -float(V * (4 * QB * QUARTERS + r)), R("cr"))
+    mset(T.selx[:], 1.0 / V, R("selx"))
+
+    def select(name, rows, fill, pat, cmp, base, cm):
+        ap = T[name][0:rows, :]
+        if fill:
+            op("G", lambda e: e.iota(ap, [[0, SCRATCH[name][1][1]]], fill, 0, allow_small_or_imprecise_dtypes=True), (), [R(name)])
+        op("G", lambda e: e.affine_select(ap, ap, pat, cmp, 0.0, base, cm), [R(name)], [R(name)])
+    select("selx", 128, 0, [[-1, 2], [-16, 8], [0, 4]], EQ, 0, 1)
+    if QUARTERS:
+        select("hm", 4, 1, [[0, 32], [-1, 4]], EQ, 0, 1)
+        select("hc", 4, 4 * QB, [[0, 32], [-1, 4], [0, 4]], EQ, 0, 1)
+    for name in ("q4f", "q4b") if QUARTERS else ():
+        select(name, 128, 1, [[-4, 32]], GE, 0, 1)
+        select(name, 128, 0, [[4, 32]], GE, 3, -1)
+    mates = on_chip(topo, cores, r)
+    if nr:
+        mset(T.srl[:, 0:16], 0.0, R("srl", 0, 16))
+        ex = T.ex[:, 0:16 * nr]
+        iota("ex", [[32, nr], [16, 2], [-16, 8]], 16, 1, 0, 16 * nr)
+        for pat, base, cm in (([[0, 2 * nr], [-16, 8]], 0, 1), ([[0, 2 * nr], [16, 8]], 15, -1)):
+            op("G", lambda e: e.affine_select(ex, ex, pat, GE, 0.0, base, cm), [R("ex")], [R("ex")])
+    senders = [p for p in range(nr) if core in matrix_dests(topo, cores, p)]
+    got = [tokens("sra", sum(width(fan(topo, cores, p, matrix_dests(topo, cores, p)), core) for p in senders))] if senders else []
+    handed = [p for p in range(mates[0]) if cores[mates[-1]] in matrix_dests(topo, cores, p)]
+    passed = sum(len(deal(out_engines(topo, cores, p), len(mates))[0]) for p in range(mates[0]) if p not in handed)
+    if handed and r == mates[-1]:
+        need("G", got[0][0], got[0][1])
+        piece = T.srl[:, 16 + 32 * handed[0]:48 + 32 * handed[-1]]
+        for q in mates[:-1]:
+            send(cores[q], piece, piece, "srh", "lss", topo.engines(core, cores[q]))
+    elif handed:
+        passed += len(topo.engines(cores[mates[-1]], core))
+    if passed:
+        got.append(tokens("srh", passed))
+
+    parts = ((2, 0, 2), (3, 2, 3), (4, 3, 4))
+
+    def prepare():
+        for bk, u0, u1 in parts:
+            w = 256 * (u1 - u0)
+            mm(ps(bk, 0, w), T.hm[0:4, :], T.hc[0:4, 0:w], True, False, [R("hm"), R("hc")], bk)
+
+    def spread(u, name):
+        bk, u0, u1 = [p for p in parts if p[1] <= u < p[2]][0]
+        for i in range(4):
+            c0 = 256 * (u - u0)
+            mm(T["ps%d" % bk][:, c0 + i:c0 + 256:4], T[name][:, 512 * u + i:512 * u + 512:4], T.selx[:], False, i == 3 and u == u1 - 1,
+               [R(name, 512 * u, 512 * u + 512), R("selx")], bk)
+
+    def wrap(u, name, sel, at):
+        for b in range(2):
+            lo = 256 * u + 128 * b
+            mm(ps(1, at + 128 * b + 32 * u, at + 128 * b + 32 * u + 32), T[name][:, lo:lo + 128], T[sel][:], True, True,
+               [R(name, lo, lo + 128), R(sel)], 1)
+
+    def places():
+        mm(ps(6, 0, 256), T.idx[:], T.xa[:], True, False, [R("idx"), R("xa")], 6)
+        mm(ps(6, 0, 256), T.idx[:], T.xb[:], False, False, [R("idx"), R("xb")], 6)
 
     PW = V // PIECES
     served, free = serve_order(topo, cores, r), (7, 6, 0)
@@ -304,113 +455,154 @@ def rank_program(g, core, T, topo):
         E, X = ("E0", "E1") if n % 2 == 0 else ("E1", "E0")
         last = n == RO - 1
         if n:
+            rows("p1", "ed")
+        if n and not QUARTERS:
             for i in range(16):
-                mm(T.ps0[:, i:256:16], T[E][:, i:V:16], T.selx[:], True, True, [R(E), R("selx")], 0)
-            act(T.qt[:], ps(0, 0, 256), ACT.Identity, [R("cq")], [R("qt")], [0], bias=T.cq[:], scale=1.0 / V)
-            act(T.xs[:], ps(0, 0, 256), ACT.Identity, [R("cr")], [R("xs")], [0], bias=T.cr[:])
+                mm(T.ps2[:, i:256:16], T[E][:, i:V:16], T.selx[:, 0:64:4], True, True, [R(E), R("selx")], 2)
+            act(T.qt[:, 0:256], ps(2, 0, 256), ACT.Relu, [R("cq")], [R("qt", 0, 256)], [2], bias=T.cq[:])
+            act(T.xs[:, 0:256], ps(2, 0, 256), ACT.Relu, [R("cr")], [R("xs", 0, 256)], [2], bias=T.cr[:], scale=float(V))
+            for b in range(2):
+                lo, hi = 128 * b, 128 * b + 128
+                mm(ps(1, lo, hi), T.qt[:, lo:hi], T.idb[:], True, True, [R("qt", lo, hi), R("idb")], 1)
+        elif n:
+            if not nq:
+                prepare()
+                for u in range(4):
+                    spread(u, E)
+            for bk, u0, u1 in parts:
+                lo, hi = 256 * u0, 256 * u1
+                if u1 < 4:
+                    act(T.qt[:, lo:hi], ps(bk, 0, hi - lo), ACT.Relu, [R("cq")], [R("qt", lo, hi)], [bk], bias=T.cq[:])
+                else:
+                    ts(T.qt[:, lo:hi], ps(bk, 0, hi - lo), HALF - 3.0 * QB, 0.0, ADD, MAX, (), [R("qt", lo, hi)], [bk])
+                for u in range(u0, u1):
+                    wrap(u, "qt", "q4b", 0)
+            for bk, u0, u1 in parts:
+                lo, hi = 256 * u0, 256 * u1
+                act(T.xs[:, lo:hi], ps(bk, 0, hi - lo), ACT.Relu, [R("cr")], [R("xs", lo, hi)], [bk], bias=T.cr[:], scale=float(V))
         else:
-            ts(T.qt[:], T.xw[:], 1.0 / V, QB - 0.5 + 0.25 / V, MUL, ADD, [R("xw")], [R("qt")])
-        for b in range(2):
-            lo, hi = 128 * b, 128 * b + 128
-            op("T", lambda e: e.transpose(ps(1, lo, hi), T.qt[:, lo:hi], T.idb[:]), [R("qt"), R("idb")], (), [1])
-        if nq:
-            mm(ps(6, 0, 256), T.id19[:], T.xa[:], True, False, [R("id19"), R("xa")], 6)
-            mm(ps(6, 0, 256), T.id19[:], T.xb[:], False, False, [R("id19"), R("xb")], 6)
+            for b in range(2):
+                lo, hi = 128 * b, 128 * b + 128
+                mm(ps(1, lo, hi), T.qt[:, lo:hi], T.idb[:], True, True, [R("qt", lo, hi), R("idb")], 1)
+            if nq:
+                places()
+        cp(T.qb[:], ps(1, 0, 256), (), [R("qb")], [1])
 
-        def sums(k0, k1):
-            for k in range(k0, k1):
+        def sums(ks):
+            for k in ks:
                 lo, hi = 256 * k, 256 * k + 256
-                mm(ps(6, 0, 256), T.id7[:], T.rl[:, lo:hi], False, k == nq - 1, [R("rl", lo, hi), R("id7")], 6)
-        k0, prev = 0, None
+                mm(ps(6, 0, 256), T.idg[:], T.rl[:, lo:hi], False, k == ks[-1], [R("rl", lo, hi), R("idg")], 6)
+        k0 = 0
         for s, w in enumerate(stages(nq)):
-            lo, hi, bk = 256 * k0, 256 * (k0 + w), 2 + s
-            for k in range(k0, k0 + w):
-                ts(T.oh[:, 256 * k:256 * k + 256], ps(1, 0, 256), float(QB + later[k]), None, EQ, None, (), [R("oh", 256 * k, 256 * k + 256)], [1])
+            lo, hi, bk = 256 * k0, 256 * (k0 + w), (5, 0, 7, 2)[s]
+            for k in range(k0 + (s > 0), min(k0 + w + 1, nq)):
+                ts(T.oh[:, 256 * k:256 * k + 256], T.qb[:], float(QB + later[k]), None, EQ, None, [R("qb")], [R("oh", 256 * k, 256 * k + 256)])
+            if k0 + w == nq:
+                ts(T.kq[:], T.qb[:], -float(QB + r + 1), 0.0, ADD, MAX, [R("qb")], [R("kq")])
             op("V", lambda e: e.tensor_tensor_scan(T.sc[:, lo:hi], T.d0[:, 0:hi - lo], T.oh[:, lo:hi], 0.0, MUL, ADD),
                [R("oh", lo, hi), R("d0")], [R("sc", lo, hi)])
             mm(ps(bk, 0, hi - lo), T.wo[:], T.oh[:, lo:hi], True, False, [R("oh", lo, hi), R("wo")], bk)
             mm(ps(bk, 0, hi - lo), T.ws[:], T.sc[:, lo:hi], False, True, [R("sc", lo, hi), R("ws")], bk)
-            act(T.rl[:, lo:hi], ps(bk, 0, hi - lo), ACT.Relu, (), [R("rl", lo, hi)], [bk])
-            if prev:
-                sums(*prev)
-            prev, k0 = (k0, k0 + w), k0 + w
+            k0 += w
+            if k0 < nq or n == 0:
+                act(T.rl[:, lo:hi], ps(bk, 0, hi - lo), ACT.Relu, (), [R("rl", lo, hi)], [bk])
+            else:
+                ts(T.rl[:, lo:hi], ps(bk, 0, hi - lo), 0.0, None, MAX, None, (), [R("rl", lo, hi)], [bk])
         if nq:
-            sums(*prev)
-            ts(T.kq[:], ps(1, 0, 256), -float(QB + r + 1), 0.0, ADD, MAX, (), [R("kq")], [1])
+            ks = list(range(nq))
+            sums(ks[:-3] + ks[-1:] + ks[-3:-1] if n else ks)
 
         def own():
-            ts(T.own[:], ps(1, 0, 256), float(QB + r), None, EQ, None, (), [R("own")], [1])
+            ts(T.own[:], T.qb[:], float(QB + r), None, EQ, None, [R("qb")], [R("own")])
         if n:
             own()
         else:
+            act(T.sr[:], ps(3, 0, 128), ACT.Copy, (), [R("sr")], [3])
             for k in range(CHUNKS):
                 lo, hi = k * CW, (k + 1) * CW
                 cp(T.E0[:, lo:hi], T.ei[:, lo:hi], [R("ei", lo, hi)], [R("E0", lo, hi)])
         if nq:
-            ts(ps(7, 0, 256), ps(6, 0, 256), 4096.0, (1 - V) / CAP, MUL, ADD, (), [R("ps7")], [6, 7])
-            tt(T.zv[:], ps(6, 0, 256), T.kq[:], ADD, [R("kq")], [R("zv")], [6])
-            tt(T.zv[:], ps(7, 0, 256), T.zv[:], MIN, [R("zv"), R("ps7")], [R("zv")], [7])
-            ts(T.o16[:], T.zv[:], float(CAP), float(V - 1), MUL, ADD, [R("zv")], [R("o16")])
-            act(T.wl0[:, 0:LH].indirect(T.o16[:, 0:128]), T[E][:], ACT.Silu, [R(E), R("o16")], [R("wl0", 0, LH)])
-            cp(T.wl1[:, 0:LH].indirect(T.o16[:, 128:256]), T[E][:], [R(E), R("o16")], [R("wl1", 0, LH)])
-            before = [("lsq", total["lsq"])] if n else []
+            ts(ps(7, 0, 256), ps(6, 0, 256), 32768.0 / (GW * F), (1 - V) / F, MUL, ADD, (), [R("ps7")], [6, 7])
+            halves = ((128, 256), (0, 128))
+            for lo, hi in halves:
+                tt(T.zv[:, lo:hi], ps(6, lo, hi), T.kq[:, lo:hi], ADD, [R("kq")], [R("zv", lo, hi)], [6])
+            for lo, hi in halves:
+                tt(T.zv[:, lo:hi], ps(7, lo, hi), T.zv[:, lo:hi], MIN, [R("zv", lo, hi), R("ps7")], [R("zv", lo, hi)], [7])
+            for lo, hi in halves:
+                ts(T.o16[:, lo:hi], T.zv[:, lo:hi], F, float(V - 1), MUL, ADD, [R("zv", lo, hi)], [R("o16", lo, hi)])
+            act(T.wl0[:, 0:LH].indirect(T.o16[:, 0:128]), T[E][:], ACT.Silu, [R(E), R("o16", 0, 128)], [R("wl0", 0, LH)])
+            cp(T.wl1[:, 0:LH].indirect(T.o16[:, 128:256]), T[E][:], [R(E), R("o16", 128, 256)], [R("wl1", 0, LH)])
             for b in range(2):
-                wl, items = "wl%d" % b, []
-                for k in range(nq):
-                    lo = V + CAP * k
-                    items.append((T.rqb[k, b::2, :], T[wl][b::16, lo:lo + CAP], [R(wl, lo, lo + CAP)], ()))
-                tok = dmas("S" if b == 0 else "Y", "dq%d" % b, items, before)
-                need("G", tok[0], tok[1])
-            fan_out(later, lambda k: T.rqb[k], T.rland[r], "rq%d" % r, "lsq")
+                wl, q = "wl%d" % b, "S" if b == 0 else "Y"
+                if F == 1:
+                    dmas(q, "dq%d" % b, [(T.lw[b::2, 0:16 * ST], T[wl][b::16, L0:LH], [R(wl, L0, LH)], [R("lw%d" % b)])])
+                else:
+                    tok = dmas(q, "dq%d" % b, [(T.rqb[k, b::2, :], T[wl][b::16, V + CAP * k:V + CAP * k + CAP], [R(wl, L0, LH)], ())
+                                               for k in range(nq)], [("lsq", total["lsq"])] if n else [])
+                    need("G", tok[0], tok[1])
+            if F > 1:
+                fan_out(asks(topo, cores, r)[0], lambda q: T.rqb[q - r - 1], T.rland[r], "rq%d" % r, "lsq")
         if n == 0:
-            ts(T.xs[:], T.xw[:], -float(V * r), None, ADD, None, [R("xw")], [R("xs")])
+            ts(T.xs[:, 0:256], T.xw[:], -float(V * r), None, ADD, None, [R("xw")], [R("xs", 0, 256)])
             own()
+            for name, w in (("cs", 8), ("ro", ST))[:(2 if F == 1 else 1) if nq else 0]:
+                ts(T.cs[:], T.iom[:, 0:8], 1.0 / w, T.p15f[:], MUL, ADD, [R("iom"), R("p15f")], [R("cs")])
+                ts(T[name + "16"][:], T.cs[:], float(w), None, MUL, None, [R("cs")], [R(name + "16")])
 
-        def turn():
+        for k in range(4):
+            mm(ps(2 + k, 0, 512), T.sr[:], T[E][:, 512 * k:512 * k + 512], True, True, [R("sr"), R(E, 512 * k, 512 * k + 512)], 2 + k)
+
+        def permuted(k0, k1):
+            for k in range(k0, k1):
+                s = 1 if k == 0 else 0
+                act(T.win[:, 512 * k + s:512 * k + 512], ps(2 + k, s, 512), ACT.Copy, (), [R("win", 512 * k + s, 512 * k + 512)], [2 + k])
+        ahead_s = AHEAD_S if nq and nr else 4
+        permuted(0, ahead_s)
+        if n and QUARTERS:
+            for u in range(4):
+                wrap(u, "xs", "q4f", 256)
+        else:
             for b in range(2):
                 lo, hi = 128 * b, 128 * b + 128
-                op("T", lambda e: e.transpose(ps(0, 256 + lo, 256 + hi), T.xs[:, lo:hi], T.idf[:]), [R("xs"), R("idf")], (), [0])
-
-        def permute(b, name, k0, k1):
-            for k in range(k0, k1):
-                bk, lo = 2 + k, 512 * k
-                mm(ps(bk, 0, 512), T.sr[:, 128 * b:128 * b + 128], T[E][:, lo:lo + 512], True, True, [R("sr"), R(E, lo, lo + 512)], bk)
-                s = 1 if k == 0 else 0
-                act(T[name][:, lo + s:lo + 512], ps(bk, s, 512), ACT.Copy, (), [R(name, lo + s, lo + 512)], [bk])
-        if n:
-            turn()
-        permute(1, "p1", 0, 4)
-        if n == 0:
-            turn()
-        ahead_s = AHEAD_S if nq and nr else 4
-        permute(0, "win", 0, ahead_s)
+                op("T", lambda e: e.transpose(ps(1, 256 + lo, 256 + hi), T.xs[:, lo:hi], T.idf[:]), [R("xs", lo, hi), R("idf")], (), [1])
         if n == 0 and nr:
-            act(T.srf[:, 0:256 * nr], T.srl[:, 0:256 * nr], ACT.Copy, (), [R("srf", 0, 256 * nr)], (), got)
-        tt(T.lf[:], ps(0, 256, 512), T.own[:], MUL, [R("own")], [R("lf")], [0])
-        cp(T.l16[:], T.lf[:], [R("lf")], [R("l16")])
+            cp(T.ex16[:, 0:16 * nr], T.ex[:, 0:16 * nr], [R("ex")], [R("ex16")])
+            act(T.srf[:, 0:256 * nr], T.srl[:, 0:16 + 32 * nr].indirect(T.ex16[:, 0:16 * nr]), ACT.Copy, [R("srl", 0, 16), R("ex16")],
+                [R("srf", 0, 256 * nr)], (), got)
         if nq:
-            ts(T.gi[:], ps(6, 0, CAP), float(CAP), None, MUL, None, (), [R("gi")], [6])
+            ts(T.gi[:], ps(6, 0, CAP), 1.0 / GW, None, MUL, None, (), [R("gi")], [6])
             ts(T.si[:], T.gi[:], -1.0, 129.0, ADD, MUL, [R("gi")], [R("si")])
             ts(T.yv[:], T.gi[:], 4096.0, None, MUL, None, [R("gi")], [R("yv")])
             ts(T.si[:], T.si[:], 4, 127, AluOpType.arith_shift_right, AluOpType.bitwise_and, [R("si")], [R("si")])
             ts(T.rb[:], T.kq[:, 0:CAP], 2.0 * CAP, float(V), MUL, ADD, [R("kq")], [R("rb")])
+        if nq and F == 1:
+            tt(T.lr[:, 0:16 * nq], T.lw[:, 0:16 * ST].indirect(T.ro16[:, 0:nq]), T.cv[:, 0:16 * nq], ADD,
+               [R("lw0"), R("lw1"), R("ro16"), R("cv")], [R("lr")])
+            tok = ts(T.lq[:, 0:16 * nq], T.lr[:, 0:16 * nq], 0.25, float(V - 1), ADD, MIN, [R("lr")], [R("lq")], (),
+                     [("lsq", total["lsq"])] if n else [])
+            need("G", tok[0], tok[1])
+            for call in asks(topo, cores, r):
+                fan_out(call, lambda q: T.lq[:, 16 * (q - r - 1):16 * (q - r)], T.lo[:, 16 * r:16 * r + 16], "rq%d" % r, "lsq")
+        tt(T.lf[:], ps(1, 256, 512), T.own[:], MUL, [R("own")], [R("lf")], [1])
+        cp(T.l16[:], T.lf[:], [R("lf")], [R("l16")])
+        if nq:
             tt(T.av[:], T.si[:], T.rb[:], ADD, [R("si"), R("rb")], [R("av")])
             tt(T.av[:], T.av[:], T.yv[:], MIN, [R("av"), R("yv")], [R("av")])
             tt(T.av[:], T.av[:], T.lf[:, 0:CAP], MAX, [R("av"), R("lf")], [R("av")])
             cp(T.a16[:], T.av[:], [R("av")], [R("a16")])
-        if n == 0:
-            late_constants()
 
         def store(k):
             lo, hi = k * PW, (k + 1) * PW
-            dmas("Y", "st%d" % k, [(T.y[:, lo:hi], T[X][:, lo:hi], [R(X, lo, hi)], ())])
+            dmas("Y", "st%d" % k, [(T["y" if last else "ed"][:, lo:hi], T[X][:, lo:hi], [R(X, lo, hi)], [R("ed", lo, hi)])])
 
-        M = "wl1" if nq else X
+        M, P1 = "wl1" if nq else X, "p1" if n else "pi"
 
         def local(k):
             lo, hi = k * PW, (k + 1) * PW
-            tt(T[M][:, lo:hi], T.p1[:, 0:V].indirect(T.l16[:, CAP + lo // 16:CAP + hi // 16]), T[E][:, lo:hi], MAX,
-               [R("p1"), R("l16"), R(E, lo, hi)], [R(M, lo, hi)])
+            if k == 0:
+                mset(T[P1][:, 0:1], 0, R(P1, 0, 4))
+            tt(T[M][:, lo:hi], T[P1][:, 0:V].indirect(T.l16[:, CAP + lo // 16:CAP + hi // 16]), T[E][:, lo:hi], MAX,
+               [R(P1), R("l16"), R(E, lo, hi)], [R(M, lo, hi)])
         ahead = AHEAD_V if nq and nr else PIECES
         for k in range(ahead):
             local(k)
@@ -419,15 +611,17 @@ def rank_program(g, core, T, topo):
                 lo, hi = k * PW, (k + 1) * PW
                 tt(T[X][:, lo:hi], T.win[:, 0:V].indirect(T.l16[:, lo // 16:hi // 16]), T[X][:, lo:hi], MAX,
                    [R("win", 0, V), R("l16"), R(X, lo, hi)], [R(X, lo, hi)])
-                if last:
-                    store(k)
+                store(k)
 
         def gather(p):
             c0, c1 = 16 * p, 16 * p + 16
-            arr = tokens("rq%d" % p, width(p, list(range(p + 1, N))))
-            dmas("Y", "lw%d" % p, [(T.lq[:, c0:c1], T.rland[p], (), [R("lq", c0, c1)])], [arr])
-            ts(T.lo[:, c0:c1], T.lq[:, c0:c1], 0.25 - V * r, float(V - 1), ADD, MIN, [R("lq", c0, c1)], [R("lo", c0, c1)])
-            act(T.rpf[:, 16 * c0:16 * c1], T[E][:, 0:V].indirect(T.lo[:, c0:c1]), ACT.Copy, [R(E), R("lo", c0, c1)], [R("rpf", 16 * c0, 16 * c1)])
+            arr = [tokens("rq%d" % p, width(asks(topo, cores, p), core))]
+            if not direct(topo, cores, p):
+                dmas("Y", "lw%d" % p, [(T.ll[:, c0:c1], T.rland[p], (), [R("ll", c0, c1)])], arr)
+                ts(T.lo[:, c0:c1], T.ll[:, c0:c1], 0.25 - V * r, float(V - 1), ADD, MIN, [R("ll", c0, c1)], [R("lo", c0, c1)])
+                arr = []
+            act(T.rpf[:, 16 * c0:16 * c1], T[E][:, 0:V].indirect(T.lo[:, c0:c1]), ACT.Copy, [R(E), R("lo", c0, c1)],
+                [R("rpf", 16 * c0, 16 * c1)], (), arr)
             bk = free[served.index(p) % len(free)]
             for b in range(2):
                 m = 256 * p + 128 * b
@@ -439,41 +633,50 @@ def rank_program(g, core, T, topo):
             left = [("ls%d" % p, total["ls%d" % p])] if n else []
             tok = cp(T.rp[:, lo:hi], ps(bk, 0, 256), (), [R("rp", lo, hi)], [bk], left)
             need("G", tok[0], tok[1])
-            k = r - p - 1
-            send(p, T.rp[:, lo:hi], T.ld[:, 256 * k:256 * k + 256], "rp%d" % r, "ls%d" % p, reply_engines(topo, cores, r, p))
+            h, engs = relay(topo, cores, r, p), reply_engines(topo, cores, r, p)
+            if h is None:
+                k = r - p - 1
+                send(cores[p], T.rp[:, lo:hi], T.ld[:, 256 * k:256 * k + 256], "rp%d" % r, "ls%d" % p, engs)
+            else:
+                j = on_chip(topo, cores, p).index(p)
+                send(h, T.rp[:, lo:hi], T.rp[:, 256 * (2 * n + j):256 * (2 * n + j + 1)], "hi%d" % j, "ls%d" % p, engs)
         for j in range(nr + LOOK):
             if j < nr:
                 gather(served[j])
             if 0 <= j - LOOK:
                 reply(served[j - LOOK])
-        permute(0, "win", ahead_s, 4)
+        permuted(ahead_s, 4)
         for k in range(ahead, PIECES):
             local(k)
         if not nq:
             continue
+        if not last:
+            if QUARTERS:
+                prepare()
+            places()
+
         def land(k):
-            arr = tokens("rp%d" % later[k], len(reply_engines(topo, cores, later[k], r)))
+            arr = tokens("rp%d" % later[k], len(landing_engines(topo, cores, later[k], r)))
             c0 = V + 256 * k
             cp(T.win[:, c0:c0 + 256], T.ld[:, 256 * k:256 * k + 256], (), [R("win", c0, c0 + 256)], (), [arr])
 
         def fold(k):
-            c0, s0 = V + 256 * k, V + CAP * k
-            tt(T.wl1[:, s0:s0 + CAP], T.win[:, c0 + CAP:c0 + 256].indirect(T.cs16[:]), T.wl1[:, s0:s0 + CAP], MAX,
-               [R("win", c0 + CAP, c0 + 256), R("cs16"), R("wl1", s0, s0 + CAP)], [R("wl1", s0, s0 + CAP)])
-        ks = sorted(range(nq), key=lambda k: serve_order(topo, cores, later[k]).index(r))
-        for k in ks[:-2]:
+            c0, mine = V + 256 * k, T.wl1[:, L0 + k:LH:ST] if F == 1 else T.wl1[:, V + CAP * k:V + CAP * k + CAP]
+            tt(mine, T.win[:, c0 + CAP:c0 + 256].indirect(T.cs16[:]), mine, MAX,
+               [R("win", c0 + CAP, c0 + 256), R("cs16"), R("wl1", L0, LH)], [R("wl1", L0, LH)])
+        ks = sorted(range(nq), key=lambda k: (relay(topo, cores, later[k], r) is not None, serve_order(topo, cores, later[k]).index(r)))
+        for j, k in enumerate(ks):
             land(k)
-            fold(k)
-        for k in ks[-2:]:
-            land(k)
-        for k in ks[-2:]:
-            fold(k)
+            if j:
+                fold(ks[j - 1])
+        fold(ks[-1])
         for k in range(PIECES):
             lo, hi = k * PW, (k + 1) * PW
             act(T.ab[:, lo:hi], T.win[:, 0:WH].indirect(T.a16[:, lo // 16:hi // 16]), ACT.Copy, [R("win", 0, WH), R("a16")], [R("ab", lo, hi)])
             tt(T[X][:, lo:hi], T.wl1[:, 0:LH].indirect(T.o16[:, CAP + lo // 16:CAP + hi // 16]), T.ab[:, lo:hi], MAX,
                [R("wl1", 0, LH), R("o16"), R("ab", lo, hi)], [R(X, lo, hi)])
-            if last:
-                store(k)
+            store(k)
+            if hi % 512 == 0 and not last and QUARTERS:
+                spread(hi // 512 - 1, X)
     for sem in sorted(total):
         need("G", sem, total[sem])

import numpy as np
from concourse.bass import DstId, IndirectOffsetOnAxis, RemoteDMATransfer
from concourse.mybir import AluOpType, ActivationFunctionType

V, N, RO, CAP, ALL = 2048, 8, 3, 128, 128
LCOLS = V + 8 + 8 * CAP
WCOLS = V + 7 * 2 * CAP
CHUNKS, PIECES = 4, 8
LOOK = 2
AHEAD_V, AHEAD_S = 1, 4
DIRECT = 4
QUARTERS = True
QB = 160
HALF = -0.5 + 0.25 / V

SCRATCH = {
    "ei": ("sbuf", [128, V], "int32"), "E0": ("sbuf", [128, V], "float32"), "E1": ("sbuf", [128, V], "float32"),
    "xw": ("sbuf", [128, 256], "int32"), "win": ("sbuf", [128, WCOLS], "float32"), "p1": ("sbuf", [128, V], "float32"),
    "ab": ("sbuf", [128, V], "float32"),
    "wl0": ("sbuf", [128, LCOLS], "float32"), "wl1": ("sbuf", [128, LCOLS], "float32"),
    "ri": ("sbuf", [128, 2], "int32"), "rf": ("sbuf", [128, 2], "float32"), "rcol": ("sbuf", [128, 2], "float32"),
    "iom": ("sbuf", [128, 128], "float32"), "iop": ("sbuf", [128, 1], "float32"), "qb": ("sbuf", [128, 256], "bfloat16"),
    "hm": ("sbuf", [128, 128], "bfloat16"), "hc": ("sbuf", [128, 512], "bfloat16"),
    "q4f": ("sbuf", [128, 32], "float32"), "q4b": ("sbuf", [128, 32], "bfloat16"),
    "ip32": ("sbuf", [128, 1], "int32"), "im32": ("sbuf", [128, 128], "int32"),
    "p16i": ("sbuf", [128, 1], "int32"), "p15i": ("sbuf", [128, 1], "int32"),
    "p16f": ("sbuf", [128, 1], "float32"), "p15f": ("sbuf", [128, 1], "float32"),
    "cq": ("sbuf", [128, 1], "float32"), "cr": ("sbuf", [128, 1], "float32"),
    "mm": ("sbuf", [128, 128], "int32"), "mg": ("sbuf", [128, 128], "float32"), "tg": ("sbuf", [128, 128], "float32"),
    "idf": ("sbuf", [128, 128], "float32"), "id128": ("sbuf", [128, 128], "float32"), "selx": ("sbuf", [128, 64], "float32"),
    "idb": ("sbuf", [128, 128], "bfloat16"), "idg": ("sbuf", [128, 128], "bfloat16"), "idx": ("sbuf", [128, 128], "bfloat16"),
    "wo": ("sbuf", [128, 128], "bfloat16"), "ws": ("sbuf", [128, 128], "bfloat16"),
    "xa": ("sbuf", [128, 256], "bfloat16"), "xb": ("sbuf", [128, 256], "bfloat16"), "d0": ("sbuf", [128, 512], "bfloat16"),
    "oh": ("sbuf", [128, 7 * 256], "bfloat16"), "sc": ("sbuf", [128, 7 * 256], "bfloat16"), "rl": ("sbuf", [128, 7 * 256], "bfloat16"),
    "roh": ("sbuf", [128, 256], "float32"), "sr": ("sbuf", [128, 128], "float32"), "srb": ("sbuf", [128, 256], "bfloat16"),
    "co": ("sbuf", [128, 2], "float32"), "co16": ("sbuf", [128, 2], "uint16"), "sm": ("sbuf", [128, 32], "bfloat16"),
    "ex": ("sbuf", [128, 7 * 16], "float32"), "ex16": ("sbuf", [128, 7 * 16], "uint16"),
    "srl": ("sbuf", [128, 16 + 7 * 32], "bfloat16"), "srf": ("sbuf", [128, 7 * 256], "float32"),
    "xs": ("sbuf", [128, 1024], "float32"), "qt": ("sbuf", [128, 1024], "bfloat16"), "kq": ("sbuf", [128, 256], "bfloat16"),
    "own": ("sbuf", [128, 256], "bfloat16"), "lf": ("sbuf", [128, 256], "float32"), "l16": ("sbuf", [128, 256], "uint16"),
    "zv": ("sbuf", [128, 256], "float32"), "o16": ("sbuf", [128, 256], "uint16"),
    "gi": ("sbuf", [128, 128], "int32"), "si": ("sbuf", [128, 128], "int32"), "rb": ("sbuf", [128, 128], "float32"),
    "yv": ("sbuf", [128, 128], "float32"), "av": ("sbuf", [128, 128], "float32"), "a16": ("sbuf", [128, 128], "uint16"),
    "cs": ("sbuf", [128, 8], "float32"), "cs16": ("sbuf", [128, 8], "uint16"), "ro16": ("sbuf", [128, 8], "uint16"),
    "lw": ("sbuf", [128, 128], "float32"), "lr": ("sbuf", [128, 7 * 16], "float32"), "cv": ("sbuf", [128, 7 * 16], "float32"),
    "lq": ("sbuf", [128, 7 * 16], "uint16"), "lo": ("sbuf", [128, 7 * 16], "uint16"), "rpf": ("sbuf", [128, 7 * 256], "float32"),
    "rp": ("sbuf", [128, 7 * 256], "uint16"), "ld": ("sbuf", [128, 7 * 256], "uint16"),
    "ll": ("sbuf", [128, 7 * 16], "float32"), "rqb": ("dram", [7, 128, 16], "float32"), "rland": ("dram", [7, 128, 16], "float32"),
    "ed": ("dram", [128, V], "float32"), "pi": ("sbuf", [128, V], "int32"), "rix": ("sbuf", [128, 1], "int32"),
}
for _k in range(8):
    SCRATCH["ps%d" % _k] = ("psum", [128, 512], "float32")
SEMAPHORES = (["qV", "qT", "qS", "qG", "lri", "lx0", "lx1", "dq0", "dq1", "lsq", "lss", "sra", "srh"]
              + ["le%d" % k for k in range(CHUNKS)] + ["st%d" % k for k in range(PIECES)]
              + ["rq%d" % k for k in range(7)] + ["rp%d" % k for k in range(8)] + ["ls%d" % k for k in range(7)]
              + ["lw%d" % k for k in range(7)] + ["ig", "hi0", "hi1"])

ADD, MUL, MAX, MIN, EQ, LE, GE = (AluOpType.add, AluOpType.mult, AluOpType.max, AluOpType.min,
                                  AluOpType.is_equal, AluOpType.is_le, AluOpType.is_ge)
ACT = ActivationFunctionType


def out_engines(topo, cores, q):
    far = [c for c in cores if topo.chip(c) != topo.chip(cores[q])]
    return topo.engines(cores[q], far[0])


def deal(engs, n):
    w = [1] * n
    while sum(w) + min(w) <= len(engs):
        w[w.index(min(w))] *= 2
    return [engs[sum(w[:k]):sum(w[:k + 1])] for k in range(n)]


def on_chip(topo, cores, q):
    return [p for p in range(N) if topo.chip(cores[p]) == topo.chip(cores[q])]


def matrix_dests(topo, cores, p):
    out = []
    for q in range(p + 1, N):
        there = on_chip(topo, cores, q)
        if p in there:
            out.append(cores[q])
        elif q == there[-1]:
            out.append(relay(topo, cores, there[on_chip(topo, cores, p).index(p)], p) or cores[q])
    return out


def reply_engines(topo, cores, q, p):
    pool, h = out_engines(topo, cores, q), relay(topo, cores, q, p)
    to = cores[p] if h is None else h
    if topo.chip(to) == topo.chip(cores[q]) and on_chip(topo, cores, q)[0] > 0:
        return [e for e in topo.engines(cores[q], to) if e not in pool]
    return pool


def fan(topo, cores, p, dests):
    pool = out_engines(topo, cores, p)
    far = sorted((q for q in dests if topo.chip(q) != topo.chip(cores[p])), reverse=True)
    near = [q for q in dests if q not in far]
    if not far:
        return [list(zip(near, deal(pool, len(near))))]
    most = len(pool) // 2
    calls = [list(zip(far[k:k + most], deal(pool, len(far[k:k + most])))) for k in range(0, len(far), most)]
    for q in near:
        calls[0].append((q, [e for e in topo.engines(cores[p], q) if e not in pool][:most]))
    return calls


def width(calls, to):
    return [len(engs) for call in calls for c, engs in call if c == to][0]


def direct(topo, cores, p):
    return sum(q not in on_chip(topo, cores, p) for q in range(p + 1, N)) <= DIRECT


def asks(topo, cores, p):
    later = list(cores[p + 1:])
    if direct(topo, cores, p):
        return fan(topo, cores, p, later)
    return [list(zip(later, deal(out_engines(topo, cores, p), len(later))))]


def serve_order(topo, cores, q):
    return sorted(range(q), key=lambda p: (p in on_chip(topo, cores, q), on_chip(topo, cores, p).index(p), p))


def relay(topo, cores, q, p):
    to = topo.chip(cores[p])
    chips = sorted({topo.chip(c) for c in cores[p + 1:]} - {to}, key=lambda c: (not topo.same_plane(c, to), -c))
    if topo.chip(cores[q]) == to:
        return None
    way = chips.index(topo.chip(cores[q]))
    if way == 0:
        return None
    if way == 1:
        near = [c for c in topo.cores_of(cores[q]) if topo.die(c) != topo.die(cores[q])]
    else:
        near = [c for c in range(ALL) if topo.mates(topo.chip(c), to) and topo.die(c) == topo.die(cores[q])]
    near = [c for c in near if c not in cores and topo.may_write(c, cores[p]) and topo.may_write(cores[q], c)]
    return near[on_chip(topo, cores, q).index(q)]


def landing_engines(topo, cores, q, p):
    h = relay(topo, cores, q, p)
    return reply_engines(topo, cores, q, p) if h is None else topo.engines(h, cores[p])


def hand_on(g, core, T, topo):
    cores, left = T.cores, 0
    jobs = [(q, p) for q in range(N) for p in serve_order(topo, cores, q) if relay(topo, cores, q, p) == core]
    for p in range(N):
        if core in matrix_dests(topo, cores, p):
            g.wait_ge(T.sem.sra, width(fan(topo, cores, p, matrix_dests(topo, cores, p)), core))
            there, piece, transfers = on_chip(topo, cores, jobs[0][0]), T.srl[:, 16 + 32 * p:48 + 32 * p], []
            for q, engs in zip(there, deal(topo.engines(core, cores[p]), len(there))):
                rid, pid, _s = topo.addr(cores[q])
                transfers.append(RemoteDMATransfer(dst_ids=[DstId(rid=rid, pnc=pid)], dma_engine_mask=sum(1 << e for e in engs),
                                                   remote_sem=T.sem.srh, src=piece, dst=piece, alu_op=0))
                left += len(engs)
            g.remote_dma_fused(transfers, local_sem=T.sem.lss)
    for n in range(RO):
        for q, p in jobs:
            j, k, engs = on_chip(topo, cores, p).index(p), q - p - 1, topo.engines(core, cores[p])
            g.wait_ge(T.sem["hi%d" % j], (n + 1) * len(reply_engines(topo, cores, q, p)))
            rid, pid, _s = topo.addr(cores[p])
            c0 = 256 * (2 * n + j)
            g.remote_dma(out_ap=T.ld[:, 256 * k:256 * k + 256], in_ap=T.rp[:, c0:c0 + 256], remote_sem=T.sem["rp%d" % q],
                         local_sem=T.sem.lss, pid=pid, routing_id=rid, dma_engine_mask=sum(1 << e for e in engs))
            left += len(engs)
    if left:
        g.wait_ge(T.sem.lss, left)


def stages(n):
    return ([1] if n % 2 == 0 else []) + [2] * ((n - 1) // 2) + [1] if n else []


def rank_program(g, core, T, topo):
    r = T.rank_of(core)
    if r is None:
        return hand_on(g, core, T, topo)
    cores = T.cores
    later = list(range(r + 1, N))
    nq, nr = len(later), r
    Q = {"V": g.vector, "T": g.tensor, "S": g.scalar, "Y": g.sync, "G": g}
    total, clock, snap, acc, bank = {}, {q: {} for q in Q}, {}, {}, {}

    def need(q, sem, val):
        ck = clock[q]
        if ck.get(sem, 0) >= val:
            return
        Q[q].wait_ge(T.sem[sem], val)
        ck[sem] = val
        for k, v in snap.get((sem, val), {}).items():
            if ck.get(k, 0) < v:
                ck[k] = v

    def order(q, reads, writes, banks, extra):
        want = {}

        def add(tok):
            if want.get(tok[0], 0) < tok[1]:
                want[tok[0]] = tok[1]
        for (b, lo, hi) in reads:
            for e in acc.get(b, []):
                if e[4] and e[0] < hi and lo < e[1]:
                    add(e[2])
        for (b, lo, hi) in writes:
            for e in acc.get(b, []):
                if e[0] < hi and lo < e[1]:
                    add(e[2])
        for k in banks:
            for oq, tok in bank.get(k, {}).items():
                if oq != q:
                    add(tok)
        for tok in extra:
            add(tok)
        for sem in sorted(want, key=lambda s: (s[0] != "q", s)):
            need(q, sem, want[sem])

    def note(q, tok, reads, writes, banks):
        s = dict(clock[q])
        s[tok[0]] = tok[1]
        snap[tok] = s
        for (b, lo, hi) in writes:
            keep = [e for e in acc.get(b, []) if not (lo <= e[0] and e[1] <= hi)]
            keep.append((lo, hi, tok, q, True))
            acc[b] = keep
        for (b, lo, hi) in reads:
            keep = [e for e in acc.get(b, []) if e[4] or e[3] != q or (e[0], e[1]) != (lo, hi) or e[2][0] != tok[0]]
            keep.append((lo, hi, tok, q, False))
            acc[b] = keep
        for k in banks:
            bank.setdefault(k, {})[q] = tok

    def op(q, fn, reads=(), writes=(), banks=(), extra=()):
        order(q, reads, writes, banks, extra)
        sem = "q" + q
        total[sem] = total.get(sem, 0) + 1
        fn(Q[q]).then_inc(T.sem[sem], 1)
        note(q, (sem, total[sem]), reads, writes, banks)
        return (sem, total[sem])

    def dmas(q, sem, items, extra=()):
        tok = (sem, total.get(sem, 0) + 16 * len(items))
        total[sem] = tok[1]
        for (o, i, rd, wr) in items:
            order(q, rd, wr, (), extra)
            Q[q].dma_start(o, i).then_inc(T.sem[sem], 16)
        for (o, i, rd, wr) in items:
            note(q, tok, rd, wr, ())
        return tok

    def tokens(sem, n):
        total[sem] = total.get(sem, 0) + n
        return (sem, total[sem])

    def ps(k, lo, hi):
        return T["ps%d" % k][:, lo:hi]

    def rem_mask(engs):
        m = 0
        for e in engs:
            m |= 1 << e
        return m

    def R(name, lo=0, hi=1 << 20):
        return (name, lo, min(hi, SCRATCH[name][1][-1]) if name in SCRATCH else hi)

    def fan_out(call, src, dst, remote, local):
        transfers = []
        for c, engs in call:
            rid, pid, _s = topo.addr(c)
            transfers.append(RemoteDMATransfer(dst_ids=[DstId(rid=rid, pnc=pid)], dma_engine_mask=rem_mask(engs),
                                               remote_sem=T.sem[remote], src=src(T.rank_of(c)), dst=dst, alu_op=0))
            tokens(local, len(engs))
        g.remote_dma_fused(transfers, local_sem=T.sem[local])

    def send(to, src, dst, remote, local, engs):
        rid, pid, _s = topo.addr(to)
        g.remote_dma(out_ap=dst, in_ap=src, remote_sem=T.sem[remote], local_sem=T.sem[local], pid=pid, routing_id=rid,
                     dma_engine_mask=rem_mask(engs))
        tokens(local, len(engs))

    CW = V // CHUNKS
    dmas("S", "lri", [(T.ri[:], T.rights[:], (), [R("ri")])])
    for b in range(2):
        dmas("Y" if b == 0 else "S", "lx%d" % b,
             [(T.xw[:, 128 * b + 16 * s:128 * b + 16 * s + 16], T.ends[16 * s + b:16 * s + b + 1, :], (),
               [R("xw", 128 * b + 16 * s, 128 * b + 16 * s + 16)]) for s in range(8)])
    for k in range(CHUNKS):
        lo, hi = k * CW, (k + 1) * CW
        dmas("Y" if k % 2 == 0 else "S", "le%d" % k, [(T.ei[:, lo:hi], T.ends[:, lo:hi], (), [R("ei", lo, hi)])])

    def iota(name, pat, base, cm, lo, hi, f32=True):
        if f32:
            op("G", lambda e: e.iota(T[name][:, lo:hi], pat, base, cm, allow_small_or_imprecise_dtypes=True), (), [(name, lo, hi)])
        else:
            op("G", lambda e: e.iota(T[name][:, lo:hi], pat, base, cm), (), [(name, lo, hi)])

    def ts(out, i, s1, s2, op0, op1, reads, writes, banks=(), extra=()):
        if op1 is None:
            return op("V", lambda e: e.tensor_scalar(out, i, s1, None, op0), reads, writes, banks, extra)
        return op("V", lambda e: e.tensor_scalar(out, i, s1, s2, op0, op1), reads, writes, banks, extra)

    def tt(out, i0, i1, o, reads, writes, banks=()):
        return op("V", lambda e: e.tensor_tensor(out, i0, i1, o), reads, writes, banks)

    def cp(out, i, reads, writes, banks=(), extra=()):
        return op("V", lambda e: e.tensor_copy(out, i), reads, writes, banks, extra)

    def act(out, i, f, reads, writes, banks=(), extra=(), **kw):
        return op("S", lambda e: e.activation(out, i, f, **kw), reads, writes, banks, extra)

    def mm(out, lhs, rhs, start, stop, reads, bk):
        return op("T", lambda e: e.matmul(out, lhs, rhs, start, stop), reads, (), [bk])

    def mset(ap, val, wr):
        op("V", lambda e: e.memset(ap, val), (), [wr])

    if direct(topo, cores, r):
        ST = 1 << max(nq - 1, 0).bit_length()
        GW, F, L0 = float(ST), 1.0, V - 1 + ST
    else:
        ST, GW, F, L0 = nq, 1.0 / CAP, float(CAP), V
    LH, WH = L0 + CAP * ST, V + 2 * CAP * nq
    iota("iop", [[1, 1]], 0, 1, 0, 1)
    iota("ip32", [[1, 1]], 0, 1, 0, 1, False)
    iota("iom", [[1, 128]], 0, 0, 0, 128)
    if nq:
        iota("im32", [[1, 128]], 0, 0, 0, 128, False)
        iota("xa", [[0, 2], [16, 128]], 0, 0, 0, 256)
        mset(T.d0[:], 1.0, R("d0"))
        mset(T.d0[:, 0:512:CAP], 0.0, R("d0"))
    iota("win", [[0, 1]], 0, 0, 0, 1)
    ts(T.p16i[:], T.ip32[:], 112, None, AluOpType.bitwise_and, None, [R("ip32")], [R("p16i")])
    ts(T.p15i[:], T.ip32[:], 15, None, AluOpType.bitwise_and, None, [R("ip32")], [R("p15i")])
    cp(T.p16f[:], T.p16i[:], [R("p16i")], [R("p16f")])
    cp(T.p15f[:], T.p15i[:], [R("p15i")], [R("p15f")])
    ts(T.idf[:], T.iom[:], T.iop[:], None, EQ, None, [R("iom"), R("iop")], [R("idf")])
    act(T.idb[:], T.idf[:], ACT.Copy, [R("idf")], [R("idb")])
    if nq:
        ts(T.mm[:], T.im32[:], 112, None, AluOpType.bitwise_and, None, [R("im32")], [R("mm")])
        ts(T.tg[:], T.iom[:], T.iop[:], None, LE, None, [R("iom"), R("iop")], [R("tg")])
        ts(T.mg[:], T.mm[:], T.p16f[:], None, EQ, None, [R("mm"), R("p16f")], [R("mg")])
    cp(T.rf[:], T.ri[:], [R("ri")], [R("rf")])
    if nq:
        ts(T.id128[:], T.idf[:], 128.0, None, MUL, None, [R("idf")], [R("id128")])
    ts(T.rcol[:], T.rf[:], T.p16f[:], None, ADD, None, [R("rf"), R("p16f")], [R("rcol")])
    if nq:
        iota("co", [[128, 2]], 0, 1, 0, 2)
        cp(T.co16[:], T.co[:], [R("co")], [R("co16")])
    for b in range(2):
        lo, hi = 128 * b, 128 * b + 128
        ts(T.roh[:, lo:hi], T.iom[:], T.rcol[:, b:b + 1], None, EQ, None, [R("iom"), R("rcol")], [R("roh", lo, hi)])
    for b in range(2):
        lo, hi = 128 * b, 128 * b + 128
        op("T", lambda e: e.transpose(ps(3, lo, hi), T.roh[:, lo:hi], T.idf[:]), [R("roh", lo, hi), R("idf")], (), [3])
    if nq:
        act(T.idx[:], T.idf[:], ACT.Copy, [R("idf")], [R("idx")], scale=GW * 2.0 ** -15)
        act(T.xb[:], T.xa[:], ACT.Identity, [R("xa"), R("p15f")], [R("xb")], bias=T.p15f[:], scale=0.0)
        act(T.srb[:], ps(3, 0, 256), ACT.Copy, (), [R("srb")], [3])
        act(T.sm[:], T.srb[:].indirect(T.co16[:]), ACT.Copy, [R("srb"), R("co16")], [R("sm")])
        act(T.ws[:], T.mg[:], ACT.Copy, [R("mg")], [R("ws")], scale=-1.0)
        act(T.idg[:], T.idf[:], ACT.Copy, [R("idf")], [R("idg")], scale=GW)
        tt(T.tg[:], T.tg[:], T.mg[:], MUL, [R("tg"), R("mg")], [R("tg")])
    cp(T.rix[:], T.rcol[:, 1:2], [R("rcol")], [R("rix")])
    if nq:
        tt(T.wo[:], T.id128[:], T.tg[:], ADD, [R("id128"), R("tg")], [R("wo")])
        for lo in range(V, LH, 512):
            hi = min(lo + 512, LH)
            act(T.wl0[:, lo:hi], T.d0[:, 0:hi - lo], ACT.Silu, [R("d0")], [R("wl0", lo, hi)])
        order("G", [R("sm")], (), (), ())
        for call in fan(topo, cores, r, matrix_dests(topo, cores, r)):
            fan_out(call, lambda q: T.sm[:], T.srl[:, 16 + 32 * r:48 + 32 * r], "sra", "lss")

    def rows(name, src):
        reads, writes = [R("rix"), (src, 0, V)], [R(name)]
        order("G", reads, writes, (), ())
        g.indirect_dma_start(T[name][:], None, T[src][:], IndirectOffsetOnAxis(ap=T.rix[:], axis=0), bounds_check=127).then_inc(T.sem.ig, 16)
        note("G", tokens("ig", 16), reads, writes, ())
    rows("pi", "ends")
    ts(T.qt[:, 0:256], T.xw[:], 1.0 / V, QB + HALF, MUL, ADD, [R("xw")], [R("qt", 0, 256)])
    if nq:
        iota("wl1", [[0, LH - V]], 0, 0, V, LH)
        if F == 1:
            iota("cv", [[-V, nq], [0, 16]], -V * (r + 1), 0, 0, 16 * nq)
    mset(T.cq[:], HALF - 3.0 * QB if QUARTERS else HALF + QB, R("cq"))
    mset(T.cr[:], -float(V * (4 * QB * QUARTERS + r)), R("cr"))
    mset(T.selx[:], 1.0 / V, R("selx"))

    def select(name, rows, fill, pat, cmp, base, cm):
        ap = T[name][0:rows, :]
        if fill:
            op("G", lambda e: e.iota(ap, [[0, SCRATCH[name][1][1]]], fill, 0, allow_small_or_imprecise_dtypes=True), (), [R(name)])
        op("G", lambda e: e.affine_select(ap, ap, pat, cmp, 0.0, base, cm), [R(name)], [R(name)])
    select("selx", 128, 0, [[-1, 2], [-16, 8], [0, 4]], EQ, 0, 1)
    if QUARTERS:
        select("hm", 4, 1, [[0, 32], [-1, 4]], EQ, 0, 1)
        select("hc", 4, 4 * QB, [[0, 32], [-1, 4], [0, 4]], EQ, 0, 1)
    for name in ("q4f", "q4b") if QUARTERS else ():
        select(name, 128, 1, [[-4, 32]], GE, 0, 1)
        select(name, 128, 0, [[4, 32]], GE, 3, -1)
    mates = on_chip(topo, cores, r)
    if nr:
        mset(T.srl[:, 0:16], 0.0, R("srl", 0, 16))
        ex = T.ex[:, 0:16 * nr]
        iota("ex", [[32, nr], [16, 2], [-16, 8]], 16, 1, 0, 16 * nr)
        for pat, base, cm in (([[0, 2 * nr], [-16, 8]], 0, 1), ([[0, 2 * nr], [16, 8]], 15, -1)):
            op("G", lambda e: e.affine_select(ex, ex, pat, GE, 0.0, base, cm), [R("ex")], [R("ex")])
    senders = [p for p in range(nr) if core in matrix_dests(topo, cores, p)]
    got = [tokens("sra", sum(width(fan(topo, cores, p, matrix_dests(topo, cores, p)), core) for p in senders))] if senders else []
    handed = [p for p in range(mates[0]) if cores[mates[-1]] in matrix_dests(topo, cores, p)]
    passed = sum(len(deal(out_engines(topo, cores, p), len(mates))[0]) for p in range(mates[0]) if p not in handed)
    if handed and r == mates[-1]:
        need("G", got[0][0], got[0][1])
        piece = T.srl[:, 16 + 32 * handed[0]:48 + 32 * handed[-1]]
        for q in mates[:-1]:
            send(cores[q], piece, piece, "srh", "lss", topo.engines(core, cores[q]))
    elif handed:
        passed += len(topo.engines(cores[mates[-1]], core))
    if passed:
        got.append(tokens("srh", passed))

    parts = ((2, 0, 2), (3, 2, 3), (4, 3, 4))

    def prepare():
        for bk, u0, u1 in parts:
            w = 256 * (u1 - u0)
            mm(ps(bk, 0, w), T.hm[0:4, :], T.hc[0:4, 0:w], True, False, [R("hm"), R("hc")], bk)

    def spread(u, name):
        bk, u0, u1 = [p for p in parts if p[1] <= u < p[2]][0]
        for i in range(4):
            c0 = 256 * (u - u0)
            mm(T["ps%d" % bk][:, c0 + i:c0 + 256:4], T[name][:, 512 * u + i:512 * u + 512:4], T.selx[:], False, i == 3 and u == u1 - 1,
               [R(name, 512 * u, 512 * u + 512), R("selx")], bk)

    def wrap(u, name, sel, at):
        for b in range(2):
            lo = 256 * u + 128 * b
            mm(ps(1, at + 128 * b + 32 * u, at + 128 * b + 32 * u + 32), T[name][:, lo:lo + 128], T[sel][:], True, True,
               [R(name, lo, lo + 128), R(sel)], 1)

    def places():
        mm(ps(6, 0, 256), T.idx[:], T.xa[:], True, False, [R("idx"), R("xa")], 6)
        mm(ps(6, 0, 256), T.idx[:], T.xb[:], False, False, [R("idx"), R("xb")], 6)

    PW = V // PIECES
    served, free = serve_order(topo, cores, r), (7, 6, 0)
    for n in range(RO):
        E, X = ("E0", "E1") if n % 2 == 0 else ("E1", "E0")
        last = n == RO - 1
        if n:
            rows("p1", "ed")
        if n and not QUARTERS:
            for i in range(16):
                mm(T.ps2[:, i:256:16], T[E][:, i:V:16], T.selx[:, 0:64:4], True, True, [R(E), R("selx")], 2)
            act(T.qt[:, 0:256], ps(2, 0, 256), ACT.Relu, [R("cq")], [R("qt", 0, 256)], [2], bias=T.cq[:])
            act(T.xs[:, 0:256], ps(2, 0, 256), ACT.Relu, [R("cr")], [R("xs", 0, 256)], [2], bias=T.cr[:], scale=float(V))
            for b in range(2):
                lo, hi = 128 * b, 128 * b + 128
                mm(ps(1, lo, hi), T.qt[:, lo:hi], T.idb[:], True, True, [R("qt", lo, hi), R("idb")], 1)
        elif n:
            if not nq:
                prepare()
                for u in range(4):
                    spread(u, E)
            for bk, u0, u1 in parts:
                lo, hi = 256 * u0, 256 * u1
                if u1 < 4:
                    act(T.qt[:, lo:hi], ps(bk, 0, hi - lo), ACT.Relu, [R("cq")], [R("qt", lo, hi)], [bk], bias=T.cq[:])
                else:
                    ts(T.qt[:, lo:hi], ps(bk, 0, hi - lo), HALF - 3.0 * QB, 0.0, ADD, MAX, (), [R("qt", lo, hi)], [bk])
                for u in range(u0, u1):
                    wrap(u, "qt", "q4b", 0)
            for bk, u0, u1 in parts:
                lo, hi = 256 * u0, 256 * u1
                act(T.xs[:, lo:hi], ps(bk, 0, hi - lo), ACT.Relu, [R("cr")], [R("xs", lo, hi)], [bk], bias=T.cr[:], scale=float(V))
        else:
            for b in range(2):
                lo, hi = 128 * b, 128 * b + 128
                mm(ps(1, lo, hi), T.qt[:, lo:hi], T.idb[:], True, True, [R("qt", lo, hi), R("idb")], 1)
            if nq:
                places()
        cp(T.qb[:], ps(1, 0, 256), (), [R("qb")], [1])

        def sums(ks):
            for k in ks:
                lo, hi = 256 * k, 256 * k + 256
                mm(ps(6, 0, 256), T.idg[:], T.rl[:, lo:hi], False, k == ks[-1], [R("rl", lo, hi), R("idg")], 6)
        k0 = 0
        for s, w in enumerate(stages(nq)):
            lo, hi, bk = 256 * k0, 256 * (k0 + w), (5, 0, 7, 2)[s]
            for k in range(k0 + (s > 0), min(k0 + w + 1, nq)):
                ts(T.oh[:, 256 * k:256 * k + 256], T.qb[:], float(QB + later[k]), None, EQ, None, [R("qb")], [R("oh", 256 * k, 256 * k + 256)])
            if k0 + w == nq:
                ts(T.kq[:], T.qb[:], -float(QB + r + 1), 0.0, ADD, MAX, [R("qb")], [R("kq")])
            op("V", lambda e: e.tensor_tensor_scan(T.sc[:, lo:hi], T.d0[:, 0:hi - lo], T.oh[:, lo:hi], 0.0, MUL, ADD),
               [R("oh", lo, hi), R("d0")], [R("sc", lo, hi)])
            mm(ps(bk, 0, hi - lo), T.wo[:], T.oh[:, lo:hi], True, False, [R("oh", lo, hi), R("wo")], bk)
            mm(ps(bk, 0, hi - lo), T.ws[:], T.sc[:, lo:hi], False, True, [R("sc", lo, hi), R("ws")], bk)
            k0 += w
            if k0 < nq or n == 0:
                act(T.rl[:, lo:hi], ps(bk, 0, hi - lo), ACT.Relu, (), [R("rl", lo, hi)], [bk])
            else:
                ts(T.rl[:, lo:hi], ps(bk, 0, hi - lo), 0.0, None, MAX, None, (), [R("rl", lo, hi)], [bk])
        if nq:
            ks = list(range(nq))
            sums(ks[:-3] + ks[-1:] + ks[-3:-1] if n else ks)

        def own():
            ts(T.own[:], T.qb[:], float(QB + r), None, EQ, None, [R("qb")], [R("own")])
        if n:
            own()
        else:
            act(T.sr[:], ps(3, 0, 128), ACT.Copy, (), [R("sr")], [3])
            for k in range(CHUNKS):
                lo, hi = k * CW, (k + 1) * CW
                cp(T.E0[:, lo:hi], T.ei[:, lo:hi], [R("ei", lo, hi)], [R("E0", lo, hi)])
        if nq:
            ts(ps(7, 0, 256), ps(6, 0, 256), 32768.0 / (GW * F), (1 - V) / F, MUL, ADD, (), [R("ps7")], [6, 7])
            halves = ((128, 256), (0, 128))
            for lo, hi in halves:
                tt(T.zv[:, lo:hi], ps(6, lo, hi), T.kq[:, lo:hi], ADD, [R("kq")], [R("zv", lo, hi)], [6])
            for lo, hi in halves:
                tt(T.zv[:, lo:hi], ps(7, lo, hi), T.zv[:, lo:hi], MIN, [R("zv", lo, hi), R("ps7")], [R("zv", lo, hi)], [7])
            for lo, hi in halves:
                ts(T.o16[:, lo:hi], T.zv[:, lo:hi], F, float(V - 1), MUL, ADD, [R("zv", lo, hi)], [R("o16", lo, hi)])
            act(T.wl0[:, 0:LH].indirect(T.o16[:, 0:128]), T[E][:], ACT.Silu, [R(E), R("o16", 0, 128)], [R("wl0", 0, LH)])
            cp(T.wl1[:, 0:LH].indirect(T.o16[:, 128:256]), T[E][:], [R(E), R("o16", 128, 256)], [R("wl1", 0, LH)])
            for b in range(2):
                wl, q = "wl%d" % b, "S" if b == 0 else "Y"
                if F == 1:
                    dmas(q, "dq%d" % b, [(T.lw[b::2, 0:16 * ST], T[wl][b::16, L0:LH], [R(wl, L0, LH)], [R("lw%d" % b)])])
                else:
                    tok = dmas(q, "dq%d" % b, [(T.rqb[k, b::2, :], T[wl][b::16, V + CAP * k:V + CAP * k + CAP], [R(wl, L0, LH)], ())
                                               for k in range(nq)], [("lsq", total["lsq"])] if n else [])
                    need("G", tok[0], tok[1])
            if F > 1:
                fan_out(asks(topo, cores, r)[0], lambda q: T.rqb[q - r - 1], T.rland[r], "rq%d" % r, "lsq")
        if n == 0:
            ts(T.xs[:, 0:256], T.xw[:], -float(V * r), None, ADD, None, [R("xw")], [R("xs", 0, 256)])
            own()
            for name, w in (("cs", 8), ("ro", ST))[:(2 if F == 1 else 1) if nq else 0]:
                ts(T.cs[:], T.iom[:, 0:8], 1.0 / w, T.p15f[:], MUL, ADD, [R("iom"), R("p15f")], [R("cs")])
                ts(T[name + "16"][:], T.cs[:], float(w), None, MUL, None, [R("cs")], [R(name + "16")])

        for k in range(4):
            mm(ps(2 + k, 0, 512), T.sr[:], T[E][:, 512 * k:512 * k + 512], True, True, [R("sr"), R(E, 512 * k, 512 * k + 512)], 2 + k)

        def permuted(k0, k1):
            for k in range(k0, k1):
                s = 1 if k == 0 else 0
                act(T.win[:, 512 * k + s:512 * k + 512], ps(2 + k, s, 512), ACT.Copy, (), [R("win", 512 * k + s, 512 * k + 512)], [2 + k])
        ahead_s = AHEAD_S if nq and nr else 4
        permuted(0, ahead_s)
        if n and QUARTERS:
            for u in range(4):
                wrap(u, "xs", "q4f", 256)
        else:
            for b in range(2):
                lo, hi = 128 * b, 128 * b + 128
                op("T", lambda e: e.transpose(ps(1, 256 + lo, 256 + hi), T.xs[:, lo:hi], T.idf[:]), [R("xs", lo, hi), R("idf")], (), [1])
        if n == 0 and nr:
            cp(T.ex16[:, 0:16 * nr], T.ex[:, 0:16 * nr], [R("ex")], [R("ex16")])
            act(T.srf[:, 0:256 * nr], T.srl[:, 0:16 + 32 * nr].indirect(T.ex16[:, 0:16 * nr]), ACT.Copy, [R("srl", 0, 16), R("ex16")],
                [R("srf", 0, 256 * nr)], (), got)
        if nq:
            ts(T.gi[:], ps(6, 0, CAP), 1.0 / GW, None, MUL, None, (), [R("gi")], [6])
            ts(T.si[:], T.gi[:], -1.0, 129.0, ADD, MUL, [R("gi")], [R("si")])
            ts(T.yv[:], T.gi[:], 4096.0, None, MUL, None, [R("gi")], [R("yv")])
            ts(T.si[:], T.si[:], 4, 127, AluOpType.arith_shift_right, AluOpType.bitwise_and, [R("si")], [R("si")])
            ts(T.rb[:], T.kq[:, 0:CAP], 2.0 * CAP, float(V), MUL, ADD, [R("kq")], [R("rb")])
        if nq and F == 1:
            tt(T.lr[:, 0:16 * nq], T.lw[:, 0:16 * ST].indirect(T.ro16[:, 0:nq]), T.cv[:, 0:16 * nq], ADD,
               [R("lw0"), R("lw1"), R("ro16"), R("cv")], [R("lr")])
            tok = ts(T.lq[:, 0:16 * nq], T.lr[:, 0:16 * nq], 0.25, float(V - 1), ADD, MIN, [R("lr")], [R("lq")], (),
                     [("lsq", total["lsq"])] if n else [])
            need("G", tok[0], tok[1])
            for call in asks(topo, cores, r):
                fan_out(call, lambda q: T.lq[:, 16 * (q - r - 1):16 * (q - r)], T.lo[:, 16 * r:16 * r + 16], "rq%d" % r, "lsq")
        tt(T.lf[:], ps(1, 256, 512), T.own[:], MUL, [R("own")], [R("lf")], [1])
        cp(T.l16[:], T.lf[:], [R("lf")], [R("l16")])
        if nq:
            tt(T.av[:], T.si[:], T.rb[:], ADD, [R("si"), R("rb")], [R("av")])
            tt(T.av[:], T.av[:], T.yv[:], MIN, [R("av"), R("yv")], [R("av")])
            tt(T.av[:], T.av[:], T.lf[:, 0:CAP], MAX, [R("av"), R("lf")], [R("av")])
            cp(T.a16[:], T.av[:], [R("av")], [R("a16")])

        def store(k):
            lo, hi = k * PW, (k + 1) * PW
            dmas("Y", "st%d" % k, [(T["y" if last else "ed"][:, lo:hi], T[X][:, lo:hi], [R(X, lo, hi)], [R("ed", lo, hi)])])

        M, P1 = "wl1" if nq else X, "p1" if n else "pi"

        def local(k):
            lo, hi = k * PW, (k + 1) * PW
            if k == 0:
                mset(T[P1][:, 0:1], 0, R(P1, 0, 4))
            tt(T[M][:, lo:hi], T[P1][:, 0:V].indirect(T.l16[:, CAP + lo // 16:CAP + hi // 16]), T[E][:, lo:hi], MAX,
               [R(P1), R("l16"), R(E, lo, hi)], [R(M, lo, hi)])
        ahead = AHEAD_V if nq and nr else PIECES
        for k in range(ahead):
            local(k)
        if not nq:
            for k in range(PIECES):
                lo, hi = k * PW, (k + 1) * PW
                tt(T[X][:, lo:hi], T.win[:, 0:V].indirect(T.l16[:, lo // 16:hi // 16]), T[X][:, lo:hi], MAX,
                   [R("win", 0, V), R("l16"), R(X, lo, hi)], [R(X, lo, hi)])
                store(k)

        def gather(p):
            c0, c1 = 16 * p, 16 * p + 16
            arr = [tokens("rq%d" % p, width(asks(topo, cores, p), core))]
            if not direct(topo, cores, p):
                dmas("Y", "lw%d" % p, [(T.ll[:, c0:c1], T.rland[p], (), [R("ll", c0, c1)])], arr)
                ts(T.lo[:, c0:c1], T.ll[:, c0:c1], 0.25 - V * r, float(V - 1), ADD, MIN, [R("ll", c0, c1)], [R("lo", c0, c1)])
                arr = []
            act(T.rpf[:, 16 * c0:16 * c1], T[E][:, 0:V].indirect(T.lo[:, c0:c1]), ACT.Copy, [R(E), R("lo", c0, c1)],
                [R("rpf", 16 * c0, 16 * c1)], (), arr)
            bk = free[served.index(p) % len(free)]
            for b in range(2):
                m = 256 * p + 128 * b
                mm(ps(bk, 128 * b, 128 * b + 128), T.srf[:, m:m + 128], T.rpf[:, 256 * p + b:256 * p + 256:2], True, True,
                   [R("srf", m, m + 128), R("rpf", 16 * c0, 16 * c1)], bk)

        def reply(p):
            lo, hi, bk = 256 * p, 256 * p + 256, free[served.index(p) % len(free)]
            left = [("ls%d" % p, total["ls%d" % p])] if n else []
            tok = cp(T.rp[:, lo:hi], ps(bk, 0, 256), (), [R("rp", lo, hi)], [bk], left)
            need("G", tok[0], tok[1])
            h, engs = relay(topo, cores, r, p), reply_engines(topo, cores, r, p)
            if h is None:
                k = r - p - 1
                send(cores[p], T.rp[:, lo:hi], T.ld[:, 256 * k:256 * k + 256], "rp%d" % r, "ls%d" % p, engs)
            else:
                j = on_chip(topo, cores, p).index(p)
                send(h, T.rp[:, lo:hi], T.rp[:, 256 * (2 * n + j):256 * (2 * n + j + 1)], "hi%d" % j, "ls%d" % p, engs)
        for j in range(nr + LOOK):
            if j < nr:
                gather(served[j])
            if 0 <= j - LOOK:
                reply(served[j - LOOK])
        permuted(ahead_s, 4)
        for k in range(ahead, PIECES):
            local(k)
        if not nq:
            continue
        if not last:
            if QUARTERS:
                prepare()
            places()

        def land(k):
            arr = tokens("rp%d" % later[k], len(landing_engines(topo, cores, later[k], r)))
            c0 = V + 256 * k
            cp(T.win[:, c0:c0 + 256], T.ld[:, 256 * k:256 * k + 256], (), [R("win", c0, c0 + 256)], (), [arr])

        def fold(k):
            c0, mine = V + 256 * k, T.wl1[:, L0 + k:LH:ST] if F == 1 else T.wl1[:, V + CAP * k:V + CAP * k + CAP]
            tt(mine, T.win[:, c0 + CAP:c0 + 256].indirect(T.cs16[:]), mine, MAX,
               [R("win", c0 + CAP, c0 + 256), R("cs16"), R("wl1", L0, LH)], [R("wl1", L0, LH)])
        ks = sorted(range(nq), key=lambda k: (relay(topo, cores, later[k], r) is not None, serve_order(topo, cores, later[k]).index(r)))
        for j, k in enumerate(ks):
            land(k)
            if j:
                fold(ks[j - 1])
        fold(ks[-1])
        for k in range(PIECES):
            lo, hi = k * PW, (k + 1) * PW
            act(T.ab[:, lo:hi], T.win[:, 0:WH].indirect(T.a16[:, lo // 16:hi // 16]), ACT.Copy, [R("win", 0, WH), R("a16")], [R("ab", lo, hi)])
            tt(T[X][:, lo:hi], T.wl1[:, 0:LH].indirect(T.o16[:, CAP + lo // 16:CAP + hi // 16]), T.ab[:, lo:hi], MAX,
               [R("wl1", 0, LH), R("o16"), R("ab", lo, hi)], [R(X, lo, hi)])
            store(k)
            if hi % 512 == 0 and not last and QUARTERS:
                spread(hi // 512 - 1, X)
    for sem in sorted(total):
        need("G", sem, total[sem])
